import numpy as np
import ml_dtypes


def mxq(x, axis, fmt="e4m3"):
    dtype, down = {"e4m3": (ml_dtypes.float8_e4m3fn, 7), "e5m2": (ml_dtypes.float8_e5m2, 14)}[fmt]
    v = np.moveaxis(np.asarray(x, np.float32).astype(ml_dtypes.bfloat16).astype(np.float64), axis, -1)
    blocks = v.reshape(v.shape[:-1] + (-1, 32))
    amax = np.abs(blocks).max(-1, keepdims=True)
    byte = np.maximum(np.where(amax > 0, np.frexp(amax)[1] - 1 + 127, 0) - down, 1)
    scale = np.exp2(byte - 127.0)
    codes = (blocks / scale).astype(np.float32).astype(dtype).astype(np.float64)
    return np.moveaxis((codes * scale).reshape(v.shape), -1, axis)


WIDE = False


def mx_kscale(k):
    if not WIDE:
        return np.ones(k)
    levels = np.array([10, -10, 5, -5, 0])
    if k % 512:
        return np.exp2(np.random.permutation(np.resize(levels, k // 32))).repeat(32)
    a = np.empty((k // 512, 16))
    for p in range(k // 512):
        a[p, :8] = np.random.permutation(np.resize(levels, 8))
        for g in range(8):
            far = levels[np.abs(levels - a[p, g]) >= 10]
            a[p, g + 8] = far[np.random.randint(len(far))]
    return np.exp2(a.ravel()).repeat(32)


BF16 = ml_dtypes.bfloat16


def bf(x):
    return np.asarray(x, np.float32).astype(BF16)


def f64(x):
    return np.asarray(x).astype(np.float64)


E2M1 = np.array([0.0, 0.5, 1.0, 1.5, 2.0, 3.0, 4.0, 6.0, -0.0, -0.5, -1.0, -1.5, -2.0, -3.0, -4.0, -6.0])


def pack_weight(w, fmt):
    k, n = w.shape
    w = f64(bf(w)).reshape(k // 32, 32, n)
    amax = np.abs(w).max(1)
    if fmt == "e4m3":
        byte = np.frexp(amax)[1] - 1 + 127 - 7
    else:
        mant, ex = np.frexp(amax / 6.0)
        byte = np.where(mant > 0.5, ex, ex - 1) + 127
    byte = np.clip(np.where(amax > 0, byte, 1), 1, 254)
    scaled = (w * np.exp2(127.0 - byte)[:, None, :]).reshape(k, n).astype(np.float32)
    by_word = np.ascontiguousarray(scaled.reshape(k // 512, 128, 4, n).transpose(0, 1, 3, 2))
    if fmt == "e4m3":
        words = by_word.astype(ml_dtypes.float8_e4m3fn).view(np.uint8)
    else:
        c = by_word.astype(ml_dtypes.float4_e2m1fn).view(np.uint8) & 0xF
        words = c[..., 0::2] | (c[..., 1::2] << 4)
    return np.ascontiguousarray(words), np.ascontiguousarray(byte.astype(np.uint8).reshape(k // 512, 16, n))


def unpack_weight(words, scales, fmt):
    g, p, n, _ = words.shape
    if fmt == "e4m3":
        vals = np.ascontiguousarray(words).view(ml_dtypes.float8_e4m3fn).astype(np.float64)
    else:
        nib = np.empty((g, p, n, 4), np.uint8)
        nib[..., 0::2] = words & 0xF
        nib[..., 1::2] = words >> 4
        vals = E2M1[nib]
    vals = vals * np.repeat(np.exp2(scales.astype(np.float64) - 127.0), 8, axis=1)[..., None]
    return vals.transpose(0, 1, 3, 2).reshape(g * 512, n)
def pack4(w):
    words, scales = pack_weight(w, "e2m1")
    return words.reshape(words.shape[0], 128, -1), scales


def unpack4(words, scales):
    return unpack_weight(words.reshape(words.shape[0], 128, -1, 2), scales, "e2m1")


def planes(Y):
    n, m = Y.shape
    b = f64(bf(Y)).reshape(n // 32, 32, m)
    amax = np.abs(b).max(1)
    byte = np.clip(np.where(amax > 0, np.frexp(amax)[1] - 1 + 127 - 7, 1), 1, 254)
    codes = (b * np.exp2(127.0 - byte)[:, None, :]).reshape(n, m).astype(np.float32).astype(ml_dtypes.float8_e4m3fn).view(np.uint8)
    words = codes.reshape(n // 512, 128, 4, m).transpose(0, 1, 3, 2)
    return np.ascontiguousarray(words), np.ascontiguousarray(byte.astype(np.uint8).reshape(n // 512, 16, m))


B, N = 512, 1024


def log_rate(y, s, gq, hq, la, lb):
    u = mxq(y * s[None, :], 1, "e4m3")
    p = u @ gq
    q = u @ hq
    synthesis = np.exp(la[None, :] + p - y)
    degradation = np.exp(lb[None, :] + q - y)
    return synthesis - degradation


def setup_inputs():
    t = mx_kscale(N)
    y = bf(np.random.standard_normal((B, N)) * 0.3)
    s = bf((1.0 + 0.1 * np.random.standard_normal(N)) * t)
    g_words, g_scales = pack4(np.random.standard_normal((N, N)) / np.sqrt(N) / t[:, None])
    h_words, h_scales = pack4(np.random.standard_normal((N, N)) / np.sqrt(N) / t[:, None])
    return {"y": y,
            "s": s,
            "g_words": g_words,
            "g_scales": g_scales,
            "h_words": h_words,
            "h_scales": h_scales,
            "la": bf(np.random.standard_normal(N) * 0.2),
            "lb": bf(np.random.standard_normal(N) * 0.2)}


def core(y, s, g_words, g_scales, h_words, h_scales, la, lb):
    y, s, la, lb = f64(y), f64(s), f64(la), f64(lb)
    gq = unpack4(g_words, g_scales)
    hq = unpack4(h_words, h_scales)
    k1 = log_rate(y, s, gq, hq, la, lb)
    y1 = y + 0.2 * k1
    k2 = log_rate(y1, s, gq, hq, la, lb)
    return 0.5 * (k1 + k2)


def reference(y, s, g_words, g_scales, h_words, h_scales, la, lb):
    R_out = core(y, s, g_words, g_scales, h_words, h_scales, la, lb)
    words, scales = planes(R_out.T)
    return R_out, words, scales

@@ -1,0 +1,274 @@
+import math
+from contextlib import ExitStack
+
+import concourse.mybir as mybir
+from concourse.masks import make_identity
+
+F32 = mybir.dt.float32
+BF16 = mybir.dt.bfloat16
+I32 = mybir.dt.int32
+U32 = mybir.dt.uint32
+U8 = mybir.dt.uint8
+FP8X4 = mybir.dt.float8_e4m3fn_x4
+FP4X4 = mybir.dt.float4_e2m1fn_x4
+ACT = mybir.ActivationFunctionType
+ALU = mybir.AluOpType
+
+FLOPS = 4 * 2 * 512 * 1024 * 1024
+
+P = 128
+HALF = 256
+
+
+def tile_ssystemlogheunslope_x2_kernel(
+    tc, y, s, g_words, g_scales, h_words, h_scales, la, lb, out_0, out_1, out_2
+):
+    nc = tc.nc
+    out_words = out_1.rearrange("g p m t -> g p (m t)")
+    with ExitStack() as ctx:
+        keep = ctx.enter_context(tc.tile_pool(name="keep", bufs=1))
+        work = ctx.enter_context(tc.tile_pool(name="work", bufs=3))
+        psum = ctx.enter_context(tc.psum_pool(name="psum", bufs=3))
+        psum_t = ctx.enter_context(tc.psum_pool(name="psum_t", bufs=2))
+        ctx.enter_context(tc.manual_schedule())
+
+        warm = keep.tile([P, 1], F32, name="warm")
+        nc.vector.memset(warm[:], 0.0)
+        nc.scalar.activation(warm[:], warm[:], ACT.Exp)
+        vec = keep.tile([P, 3, 4, 4], BF16, name="vec")
+        for a, v in enumerate((s, la, lb)):
+            nc.scalar.dma_start(out=vec[:, a, 0:2], in_=v.rearrange("(g p t) -> p g t", p=P, t=4))
+        scale_raw = keep.tile([P, 4, 1024], U8, name="scale_raw", align_bytes=64)
+        nc.gpsimd.memset(scale_raw[:].rearrange("p a n -> p (a n)").bitcast(I32), 0)
+        ident = keep.tile([P, P], F32, name="ident")
+        make_identity(nc, ident[:])
+        y_tok = [keep.tile([P, 1024], BF16, name="y_tok%d" % r) for r in range(4)]
+        word_raw = [keep.tile([P, 2, 2048], U8, name="word_raw%d" % w, align_bytes=64) for w in range(2)]
+        for r in range(2):
+            nc.sync.dma_start(out=y_tok[r][:], in_=y[P * r : P * (r + 1), :])
+        for w, sc in enumerate((g_scales, h_scales)):
+            for q in range(4):
+                nc.scalar.dma_start(
+                    out=scale_raw[32 * q : 32 * q + 4, 2 * w : 2 * w + 2, :].bitcast(I32),
+                    in_=sc[:, 4 * q : 4 * q + 4, :].rearrange("k r n -> r k n").bitcast(I32),
+                )
+        for w, words in enumerate((g_words, h_words)):
+            for k in range(2):
+                nc.sync.dma_start(out=word_raw[w][:, k, :].bitcast(I32), in_=words[k].bitcast(I32))
+        for r in range(2, 4):
+            nc.sync.dma_start(out=y_tok[r][:], in_=y[P * r : P * (r + 1), :])
+
+        vec_f = keep.tile([P, 3, 8], F32, name="vec_f")
+        words_p = [keep.tile([P, 2, 8, 256], U8, name="words_p%d" % w, align_bytes=64) for w in range(2)]
+        scale_p = keep.tile([P, 4, 8, P], U8, name="scale_p", align_bytes=64)
+        y4 = keep.tile([P, 2, 512, 4], BF16, name="y4", align_bytes=64)
+        codes = [keep.tile([P, 2, 512], U32, name="codes%d" % i, align_bytes=64) for i in range(2)]
+        scales = [keep.tile([P, 2, 512], U8, name="scales%d" % i, align_bytes=64) for i in range(2)]
+        k1h = keep.tile([P, 8, 512], F32, name="k1h", align_bytes=64)
+        y1 = keep.tile([P, 8, 512], F32, name="y1", align_bytes=64)
+
+        def vectors():
+            nc.vector.tensor_copy(out=vec_f[:, 0], in_=vec[:, 0, 0:2].rearrange("p g t -> p (g t)"))
+            nc.vector.tensor_scalar_add(vec_f[:, 1:3], vec[:, 1:3, 0:2].rearrange("p a g t -> p a (g t)"), math.log(0.5))
+
+        def quantize(stage, grp, t0, src):
+            nc.vector.quantize_mx(
+                out=codes[stage][:, grp, t0 : t0 + HALF].bitcast(FP8X4),
+                scales=scales[stage][:, grp, t0 : t0 + HALF],
+                in_=src[:].rearrange("p n t -> p (n t)"),
+            )
+
+        def head_t(half, grp):
+            bank = psum_t.tile([P, 2, HALF], F32, name="bank", tag="tr")
+            for r in range(2):
+                yw = y_tok[2 * half + r][:].bitcast(F32)
+                for u in range(2):
+                    nc.tensor.transpose(
+                        bank[:, u, P * r : P * (r + 1)], yw[:, 256 * grp + u : 256 * (grp + 1) : 2], ident[:]
+                    )
+            t0 = HALF * half
+            nc.scalar.copy(
+                out=y4[:, grp, t0 : t0 + HALF, :].rearrange("p n t -> p (n t)").bitcast(F32).rearrange("p (n u) -> p n u", u=2),
+                in_=bank[:].rearrange("p u n -> p n u"),
+            )
+
+        def head_q(half, grp):
+            t0 = HALF * half
+            u0 = work.tile([P, HALF, 4], BF16, name="u0", tag="u_i", align_bytes=64)
+            nc.vector.tensor_tensor(
+                out=u0[:],
+                in0=y4[:, grp, t0 : t0 + HALF, :],
+                in1=vec[:, 0, grp, :].unsqueeze(1).to_broadcast([P, HALF, 4]),
+                op=ALU.mult,
+            )
+            quantize(0, grp, t0, u0)
+
+        def permute_words(slot):
+            g, t = slot // 4, slot % 4
+            for w in range(2):
+                src = word_raw[w][:].rearrange("p k (g m t b) -> p k g m t b", g=2, t=4, b=2)
+                nc.vector.tensor_copy(
+                    out=words_p[w][:, :, slot, :].rearrange("p k (m b) -> p k m b", b=2), in_=src[:, :, g, :, t, :]
+                )
+
+        def permute_scales(eng, g):
+            src = scale_raw[:].rearrange("p a (g m t) -> p a g t m", g=2, t=4)
+            eng.tensor_copy(out=scale_p[:, :, 4 * g : 4 * g + 4, :], in_=src[:, :, g])
+
+        units = [(st, pr, hf) for st in range(2) for hf in range(2) for pr in range(4)]
+        n_units = len(units)
+        live = {}
+
+        def multiply(i):
+            st, pr, hf = units[i]
+            banks = []
+            for w in range(2):
+                ps = psum.tile([P, 2, HALF], F32, name="ps%d" % w, tag="ps%d" % w)
+                for j in range(2):
+                    slot = 2 * pr + j
+                    for q in range(2):
+                        c0 = HALF * hf + P * q
+                        for k in range(2):
+                            nc.tensor.matmul_mx(
+                                out=ps[:, j, P * q : P * (q + 1)],
+                                lhsT=words_p[w][:, k, slot, :].bitcast(FP4X4),
+                                lhsT_scale=scale_p[:, 2 * w + k, slot, :],
+                                rhs=codes[st][:, k, c0 : c0 + P].bitcast(FP8X4),
+                                rhs_scale=scales[st][:, k, c0 : c0 + P],
+                                start=(k == 0),
+                                stop=(k == 1),
+                            )
+                banks.append(ps)
+            live[i] = {"ps": banks}
+
+        def y_view(i):
+            st, pr, hf = units[i]
+            t0 = HALF * hf
+            if st == 0:
+                a = 2 * (pr % 2)
+                return y4[:, pr // 2, t0 : t0 + HALF, a : a + 2].rearrange("p n t -> p t n")
+            return y1[:, 2 * pr : 2 * pr + 2, t0 : t0 + HALF]
+
+        def subtract_y(i):
+            ar = work.tile([P, 2, 2, HALF], F32, name="ar", tag="ar")
+            for w in range(2):
+                nc.vector.tensor_tensor(out=ar[:, w], in0=live[i]["ps"][w][:], in1=y_view(i), op=ALU.subtract)
+            live[i]["ar"] = ar
+
+        def exps(i):
+            st, pr, hf = units[i]
+            ex = work.tile([P, 2, 2, HALF], F32, name="ex", tag="ex")
+            for w in range(2):
+                for j in range(2):
+                    slot = 2 * pr + j
+                    nc.scalar.activation(
+                        ex[:, w, j], live[i]["ar"][:, w, j], ACT.Exp, bias=vec_f[:, 1 + w, slot : slot + 1]
+                    )
+            live[i]["ex"] = ex
+
+        def gp(i):
+            st, pr, hf = units[i]
+            t0 = HALF * hf
+            k_view = k1h[:, 2 * pr : 2 * pr + 2, t0 : t0 + HALF]
+            ex = live[i]["ex"]
+            if st == 0:
+                nc.gpsimd.tensor_tensor(out=k_view, in0=ex[:, 0], in1=ex[:, 1], op=ALU.subtract)
+            else:
+                tt = work.tile([P, 2, HALF], F32, name="tt", tag="tt")
+                nc.gpsimd.tensor_tensor(out=tt[:], in0=k_view, in1=ex[:, 0], op=ALU.add)
+                live[i]["tt"] = tt
+
+        def after(i):
+            st, pr, hf = units[i]
+            t0 = HALF * hf
+            if st == 0:
+                nc.vector.scalar_tensor_tensor(
+                    out=y1[:, 2 * pr : 2 * pr + 2, t0 : t0 + HALF],
+                    in0=k1h[:, 2 * pr : 2 * pr + 2, t0 : t0 + HALF],
+                    scalar=0.4,
+                    in1=y_view(i),
+                    op0=ALU.mult,
+                    op1=ALU.add,
+                )
+                if pr % 2 == 0:
+                    live["u1s"] = work.tile([P, 4, HALF], BF16, name="u1s", tag="u1s")
+                for j in range(2):
+                    slot = 2 * pr + j
+                    nc.scalar.activation(
+                        live["u1s"][:, slot % 4, :], y1[:, slot, t0 : t0 + HALF], ACT.Copy, scale=vec_f[:, 0, slot : slot + 1]
+                    )
+            else:
+                if pr % 2 == 0:
+                    live["o"] = work.tile([P, 4, HALF], F32, name="o", tag="o")
+                a = 2 * (pr % 2)
+                nc.vector.tensor_tensor(out=live["o"][:, a : a + 2, :], in0=live[i]["tt"][:], in1=live[i]["ex"][:, 1], op=ALU.subtract)
+                if pr % 2 == 1:
+                    o = live["o"]
+                    for r in range(2):
+                        bank = psum_t.tile([P, 4, P], F32, name="obank", tag="tr")
+                        for t in range(4):
+                            nc.tensor.transpose(bank[:, t, :], o[:, t, P * r : P * (r + 1)], ident[:])
+                        orow = work.tile([P, P, 4], F32, name="orow", tag="orow")
+                        nc.scalar.copy(out=orow[:], in_=bank[:].rearrange("p t m -> p m t"))
+                        r0 = t0 + P * r
+                        c0 = 512 * (pr // 2)
+                        nc.sync.dma_start(out=out_0[r0 : r0 + P, c0 : c0 + 512], in_=orow[:].rearrange("p m t -> p (m t)"))
+
+        def late(i):
+            st, pr, hf = units[i]
+            if pr % 2 == 0:
+                return
+            t0 = HALF * hf
+            grp = pr // 2
+            if st == 0:
+                u1 = work.tile([P, HALF, 4], BF16, name="u1", tag="u_i", align_bytes=64)
+                nc.vector.tensor_copy(out=u1[:], in_=live["u1s"][:].rearrange("p t n -> p n t"))
+                quantize(1, grp, t0, u1)
+            else:
+                ob = work.tile([P, HALF, 4], BF16, name="ob", tag="u_i", align_bytes=64)
+                nc.vector.tensor_copy(out=ob[:], in_=live["o"][:].rearrange("p t n -> p n t"))
+                oc = work.tile([P, HALF], U32, name="oc", tag="oc", align_bytes=64)
+                osc = work.tile([P, HALF], U8, name="osc", tag="osc", align_bytes=64)
+                nc.vector.quantize_mx(out=oc[:].bitcast(FP8X4), scales=osc[:], in_=ob[:].rearrange("p n t -> p (n t)"))
+                nc.sync.dma_start(out=out_words[grp][:, 4 * t0 : 4 * (t0 + HALF)].bitcast(I32), in_=oc[:].bitcast(I32))
+                for q in range(4):
+                    nc.sync.dma_start(
+                        out=out_2[grp, 4 * q : 4 * q + 4, t0 : t0 + HALF].bitcast(I32),
+                        in_=osc[32 * q : 32 * q + 4, :].bitcast(I32),
+                    )
+
+        vectors()
+        for grp in range(2):
+            head_t(0, grp)
+        for grp in range(2):
+            head_q(0, grp)
+        permute_scales(nc.gpsimd, 0)
+        permute_words(0)
+        permute_words(1)
+        multiply(0)
+        permute_scales(nc.gpsimd, 1)
+        permute_words(2)
+        permute_words(3)
+        multiply(1)
+        for i in range(n_units + 2):
+            if i < n_units:
+                subtract_y(i)
+                exps(i)
+                gp(i)
+            if i == 0:
+                for slot in range(4, 6):
+                    permute_words(slot)
+            if i == 1:
+                for slot in range(6, 8):
+                    permute_words(slot)
+                for grp in range(2):
+                    head_t(1, grp)
+            if i == 2:
+                for grp in range(2):
+                    head_q(1, grp)
+            if i + 2 < n_units:
+                multiply(i + 2)
+            if i >= 2 and i - 2 < n_units:
+                late(i - 2)
+            if 1 <= i <= n_units:
+                after(i - 1)

@@ -18,6 +18,11 @@ FLOPS = 4 * 2 * 512 * 1024 * 1024
 
 P = 128
 HALF = 256
+ON_S = (9,)
+ON_V = (15,)
+LAG = {3: 1, 7: 1, 14: 1, 15: 1}
+SX = {}
+IX = {13: 1}
 
 
 def tile_ssystemlogheunslope_x2_kernel(
@@ -32,31 +37,38 @@ def tile_ssystemlogheunslope_x2_kernel(
         psum_t = ctx.enter_context(tc.psum_pool(name="psum_t", bufs=2))
         ctx.enter_context(tc.manual_schedule())
 
-        warm = keep.tile([P, 1], F32, name="warm")
-        nc.vector.memset(warm[:], 0.0)
-        nc.scalar.activation(warm[:], warm[:], ACT.Exp)
         vec = keep.tile([P, 3, 4, 4], BF16, name="vec")
         for a, v in enumerate((s, la, lb)):
             nc.scalar.dma_start(out=vec[:, a, 0:2], in_=v.rearrange("(g p t) -> p g t", p=P, t=4))
         scale_raw = keep.tile([P, 4, 1024], U8, name="scale_raw", align_bytes=64)
-        nc.gpsimd.memset(scale_raw[:].rearrange("p a n -> p (a n)").bitcast(I32), 0)
+        nc.vector.memset(scale_raw[:, 0:2].rearrange("p a n -> p (a n)").bitcast(I32), 0)
+        nc.vector.memset(scale_raw[:, 2:4].rearrange("p a n -> p (a n)").bitcast(I32), 0)
         ident = keep.tile([P, P], F32, name="ident")
         make_identity(nc, ident[:])
         y_tok = [keep.tile([P, 1024], BF16, name="y_tok%d" % r) for r in range(4)]
         word_raw = [keep.tile([P, 2, 2048], U8, name="word_raw%d" % w, align_bytes=64) for w in range(2)]
+        def load_words(grp):
+            for w, words in enumerate((g_words, h_words)):
+                nc.sync.dma_start(
+                    out=word_raw[w][:, :, 1024 * grp : 1024 * (grp + 1)].bitcast(I32),
+                    in_=words[:, :, 1024 * grp : 1024 * (grp + 1)].rearrange("k p b -> p k b").bitcast(I32),
+                )
+
         for r in range(2):
             nc.sync.dma_start(out=y_tok[r][:], in_=y[P * r : P * (r + 1), :])
+        load_words(0)
+        warm = keep.tile([P, 1], F32, name="warm")
         for w, sc in enumerate((g_scales, h_scales)):
             for q in range(4):
                 nc.scalar.dma_start(
                     out=scale_raw[32 * q : 32 * q + 4, 2 * w : 2 * w + 2, :].bitcast(I32),
                     in_=sc[:, 4 * q : 4 * q + 4, :].rearrange("k r n -> r k n").bitcast(I32),
                 )
-        for w, words in enumerate((g_words, h_words)):
-            for k in range(2):
-                nc.sync.dma_start(out=word_raw[w][:, k, :].bitcast(I32), in_=words[k].bitcast(I32))
+        nc.vector.memset(warm[:], 0.0)
+        nc.scalar.activation(warm[:], warm[:], ACT.Exp)
         for r in range(2, 4):
             nc.sync.dma_start(out=y_tok[r][:], in_=y[P * r : P * (r + 1), :])
+        load_words(1)
 
         vec_f = keep.tile([P, 3, 8], F32, name="vec_f")
         words_p = [keep.tile([P, 2, 8, 256], U8, name="words_p%d" % w, align_bytes=64) for w in range(2)]
@@ -66,6 +78,8 @@ def tile_ssystemlogheunslope_x2_kernel(
         scales = [keep.tile([P, 2, 512], U8, name="scales%d" % i, align_bytes=64) for i in range(2)]
         k1h = keep.tile([P, 8, 512], F32, name="k1h", align_bytes=64)
         y1 = keep.tile([P, 8, 512], F32, name="y1", align_bytes=64)
+
+        live = {}
 
         def vectors():
             nc.vector.tensor_copy(out=vec_f[:, 0], in_=vec[:, 0, 0:2].rearrange("p g t -> p (g t)"))
@@ -87,21 +101,21 @@ def tile_ssystemlogheunslope_x2_kernel(
                         bank[:, u, P * r : P * (r + 1)], yw[:, 256 * grp + u : 256 * (grp + 1) : 2], ident[:]
                     )
             t0 = HALF * half
+            u0 = work.tile([P, HALF, 4], BF16, name="u0", tag="u_i", align_bytes=64)
+            nc.vector.tensor_tensor(
+                out=u0[:].rearrange("p n (u e) -> p n u e", e=2),
+                in0=bank[:].bitcast(BF16).rearrange("p u (n e) -> p n u e", e=2),
+                in1=vec[:, 0, grp, :].rearrange("p (u e) -> p u e", e=2).unsqueeze(1).to_broadcast([P, HALF, 2, 2]),
+                op=ALU.mult,
+            )
+            live["u0", half, grp] = u0
             nc.scalar.copy(
                 out=y4[:, grp, t0 : t0 + HALF, :].rearrange("p n t -> p (n t)").bitcast(F32).rearrange("p (n u) -> p n u", u=2),
                 in_=bank[:].rearrange("p u n -> p n u"),
             )
 
         def head_q(half, grp):
-            t0 = HALF * half
-            u0 = work.tile([P, HALF, 4], BF16, name="u0", tag="u_i", align_bytes=64)
-            nc.vector.tensor_tensor(
-                out=u0[:],
-                in0=y4[:, grp, t0 : t0 + HALF, :],
-                in1=vec[:, 0, grp, :].unsqueeze(1).to_broadcast([P, HALF, 4]),
-                op=ALU.mult,
-            )
-            quantize(0, grp, t0, u0)
+            quantize(0, grp, HALF * half, live["u0", half, grp])
 
         def permute_words(slot):
             g, t = slot // 4, slot % 4
@@ -111,13 +125,18 @@ def tile_ssystemlogheunslope_x2_kernel(
                     out=words_p[w][:, :, slot, :].rearrange("p k (m b) -> p k m b", b=2), in_=src[:, :, g, :, t, :]
                 )
 
-        def permute_scales(eng, g):
+        def permute_scales(w, g):
             src = scale_raw[:].rearrange("p a (g m t) -> p a g t m", g=2, t=4)
-            eng.tensor_copy(out=scale_p[:, :, 4 * g : 4 * g + 4, :], in_=src[:, :, g])
+            nc.vector.tensor_copy(
+                out=scale_p[:, 2 * w : 2 * w + 2, 4 * g : 4 * g + 4, :], in_=src[:, 2 * w : 2 * w + 2, g]
+            )
+
+        def permute_pair(pr):
+            permute_words(2 * pr)
+            permute_words(2 * pr + 1)
 
         units = [(st, pr, hf) for st in range(2) for hf in range(2) for pr in range(4)]
         n_units = len(units)
-        live = {}
 
         def multiply(i):
             st, pr, hf = units[i]
@@ -166,21 +185,22 @@ def tile_ssystemlogheunslope_x2_kernel(
                     )
             live[i]["ex"] = ex
 
-        def gp(i):
+        def difference(i, eng):
             st, pr, hf = units[i]
             t0 = HALF * hf
             k_view = k1h[:, 2 * pr : 2 * pr + 2, t0 : t0 + HALF]
             ex = live[i]["ex"]
             if st == 0:
-                nc.gpsimd.tensor_tensor(out=k_view, in0=ex[:, 0], in1=ex[:, 1], op=ALU.subtract)
+                eng.tensor_tensor(out=k_view, in0=ex[:, 0], in1=ex[:, 1], op=ALU.subtract)
             else:
                 tt = work.tile([P, 2, HALF], F32, name="tt", tag="tt")
-                nc.gpsimd.tensor_tensor(out=tt[:], in0=k_view, in1=ex[:, 0], op=ALU.add)
+                eng.tensor_tensor(out=tt[:], in0=k_view, in1=ex[:, 0], op=ALU.add)
                 live[i]["tt"] = tt
 
-        def after(i):
+        def finish_v(i):
             st, pr, hf = units[i]
             t0 = HALF * hf
+            grp = pr // 2
             if st == 0:
                 nc.vector.scalar_tensor_tensor(
                     out=y1[:, 2 * pr : 2 * pr + 2, t0 : t0 + HALF],
@@ -190,85 +210,123 @@ def tile_ssystemlogheunslope_x2_kernel(
                     op0=ALU.mult,
                     op1=ALU.add,
                 )
-                if pr % 2 == 0:
-                    live["u1s"] = work.tile([P, 4, HALF], BF16, name="u1s", tag="u1s")
-                for j in range(2):
-                    slot = 2 * pr + j
-                    nc.scalar.activation(
-                        live["u1s"][:, slot % 4, :], y1[:, slot, t0 : t0 + HALF], ACT.Copy, scale=vec_f[:, 0, slot : slot + 1]
-                    )
             else:
                 if pr % 2 == 0:
-                    live["o"] = work.tile([P, 4, HALF], F32, name="o", tag="o")
+                    live["o", hf, grp] = work.tile([P, 4, HALF], F32, name="o", tag="o")
                 a = 2 * (pr % 2)
-                nc.vector.tensor_tensor(out=live["o"][:, a : a + 2, :], in0=live[i]["tt"][:], in1=live[i]["ex"][:, 1], op=ALU.subtract)
-                if pr % 2 == 1:
-                    o = live["o"]
-                    for r in range(2):
-                        bank = psum_t.tile([P, 4, P], F32, name="obank", tag="tr")
-                        for t in range(4):
-                            nc.tensor.transpose(bank[:, t, :], o[:, t, P * r : P * (r + 1)], ident[:])
-                        orow = work.tile([P, P, 4], F32, name="orow", tag="orow")
-                        nc.scalar.copy(out=orow[:], in_=bank[:].rearrange("p t m -> p m t"))
-                        r0 = t0 + P * r
-                        c0 = 512 * (pr // 2)
-                        nc.sync.dma_start(out=out_0[r0 : r0 + P, c0 : c0 + 512], in_=orow[:].rearrange("p m t -> p (m t)"))
+                nc.vector.tensor_tensor(
+                    out=live["o", hf, grp][:, a : a + 2, :], in0=live[i]["tt"][:], in1=live[i]["ex"][:, 1], op=ALU.subtract
+                )
 
-        def late(i):
+        def finish_s(i):
             st, pr, hf = units[i]
-            if pr % 2 == 0:
-                return
             t0 = HALF * hf
             grp = pr // 2
             if st == 0:
-                u1 = work.tile([P, HALF, 4], BF16, name="u1", tag="u_i", align_bytes=64)
-                nc.vector.tensor_copy(out=u1[:], in_=live["u1s"][:].rearrange("p t n -> p n t"))
-                quantize(1, grp, t0, u1)
-            else:
-                ob = work.tile([P, HALF, 4], BF16, name="ob", tag="u_i", align_bytes=64)
-                nc.vector.tensor_copy(out=ob[:], in_=live["o"][:].rearrange("p t n -> p n t"))
-                oc = work.tile([P, HALF], U32, name="oc", tag="oc", align_bytes=64)
-                osc = work.tile([P, HALF], U8, name="osc", tag="osc", align_bytes=64)
-                nc.vector.quantize_mx(out=oc[:].bitcast(FP8X4), scales=osc[:], in_=ob[:].rearrange("p n t -> p (n t)"))
-                nc.sync.dma_start(out=out_words[grp][:, 4 * t0 : 4 * (t0 + HALF)].bitcast(I32), in_=oc[:].bitcast(I32))
-                for q in range(4):
-                    nc.sync.dma_start(
-                        out=out_2[grp, 4 * q : 4 * q + 4, t0 : t0 + HALF].bitcast(I32),
-                        in_=osc[32 * q : 32 * q + 4, :].bitcast(I32),
+                if pr % 2 == 0:
+                    live["u1s", hf, grp] = work.tile([P, 2, HALF, 2], BF16, name="u1s", tag="u1s", align_bytes=64)
+                for j in range(2):
+                    slot = 2 * pr + j
+                    nc.scalar.activation(
+                        live["u1s", hf, grp][:, (slot % 4) // 2, :, slot % 2],
+                        y1[:, slot, t0 : t0 + HALF],
+                        ACT.Copy,
+                        scale=vec_f[:, 0, slot : slot + 1],
                     )
+            elif pr % 2 == 1:
+                o = live["o", hf, grp]
+                for r in range(2):
+                    bank = psum_t.tile([P, 4, P], F32, name="obank", tag="tr")
+                    for t in range(4):
+                        nc.tensor.transpose(bank[:, t, :], o[:, t, P * r : P * (r + 1)], ident[:])
+                    orow = work.tile([P, P, 4], F32, name="orow", tag="orow", bufs=6)
+                    nc.scalar.copy(out=orow[:], in_=bank[:].rearrange("p t m -> p m t"))
+                    r0 = t0 + P * r
+                    c0 = 512 * grp
+                    (nc.scalar if i == 15 else nc.sync).dma_start(out=out_0[r0 : r0 + P, c0 : c0 + 512], in_=orow[:].rearrange("p m t -> p (m t)"))
 
+        def interleave(i, on_scalar):
+            st, pr, hf = units[i]
+            if st == 1:
+                src = live["o", hf, pr // 2][:].rearrange("p t n -> p n t")
+            ui = work.tile([P, HALF, 4], BF16, name="ui", tag="u_i", align_bytes=64)
+            if st == 0:
+                pairs = live["u1s", hf, pr // 2][:].rearrange("p u n e -> p u (n e)").bitcast(F32)
+                (nc.scalar.copy if on_scalar else nc.vector.tensor_copy)(
+                    out=ui[:].rearrange("p n t -> p (n t)").bitcast(F32).rearrange("p (n u) -> p n u", u=2),
+                    in_=pairs.rearrange("p u n -> p n u"),
+                )
+            elif on_scalar:
+                nc.scalar.copy(out=ui[:], in_=src)
+            else:
+                nc.vector.tensor_copy(out=ui[:], in_=src)
+            live[i]["ui"] = ui
+
+        def quantize_unit(i):
+            st, pr, hf = units[i]
+            t0 = HALF * hf
+            grp = pr // 2
+            ui = live[i]["ui"]
+            if st == 0:
+                quantize(1, grp, t0, ui)
+                return
+            oc = work.tile([P, HALF], U32, name="oc", tag="oc", align_bytes=64)
+            osc = work.tile([P, HALF], U8, name="osc", tag="osc", align_bytes=64)
+            nc.vector.quantize_mx(out=oc[:].bitcast(FP8X4), scales=osc[:], in_=ui[:].rearrange("p n t -> p (n t)"))
+            nc.sync.dma_start(out=out_words[grp][:, 4 * t0 : 4 * (t0 + HALF)].bitcast(I32), in_=oc[:].bitcast(I32))
+            for q in range(4):
+                nc.sync.dma_start(
+                    out=out_2[grp, 4 * q : 4 * q + 4, t0 : t0 + HALF].bitcast(I32),
+                    in_=osc[32 * q : 32 * q + 4, :].bitcast(I32),
+                )
+
+        permute_scales(0, 0)
         vectors()
         for grp in range(2):
             head_t(0, grp)
         for grp in range(2):
             head_q(0, grp)
-        permute_scales(nc.gpsimd, 0)
-        permute_words(0)
-        permute_words(1)
+        fin = [i + LAG.get(i, 2) for i in range(n_units)]
+        fin_s = [fin[i] + SX.get(i, 0) for i in range(n_units)]
+        inter = {i: fin[i] + (0 if i in ON_S else 1) + IX.get(i, 0) for i in range(1, n_units, 2)}
+        quant = {i: inter[i] + 1 for i in inter}
+        mul = [i - 2 for i in range(n_units)]
+        for i in range(8, n_units):
+            mul[i] = max(i - 2, max(quant[j] for j in ((1, 3) if i < 12 else (5, 7))))
+        permute_scales(1, 0)
+        permute_pair(0)
         multiply(0)
-        permute_scales(nc.gpsimd, 1)
-        permute_words(2)
-        permute_words(3)
+        permute_pair(1)
         multiply(1)
-        for i in range(n_units + 2):
+        for i in range(n_units + 5):
             if i < n_units:
                 subtract_y(i)
                 exps(i)
-                gp(i)
+                if i not in ON_V:
+                    difference(i, nc.gpsimd)
             if i == 0:
-                for slot in range(4, 6):
-                    permute_words(slot)
+                for w in range(2):
+                    permute_scales(w, 1)
+                permute_pair(2)
             if i == 1:
-                for slot in range(6, 8):
-                    permute_words(slot)
+                permute_pair(3)
                 for grp in range(2):
                     head_t(1, grp)
             if i == 2:
                 for grp in range(2):
                     head_q(1, grp)
-            if i + 2 < n_units:
-                multiply(i + 2)
-            if i >= 2 and i - 2 < n_units:
-                late(i - 2)
-            if 1 <= i <= n_units:
-                after(i - 1)
+            for j in range(n_units):
+                if fin[j] == i:
+                    if j in ON_V:
+                        difference(j, nc.vector)
+                    finish_v(j)
+                if fin_s[j] == i:
+                    finish_s(j)
+            for j in inter:
+                if quant[j] == i:
+                    quantize_unit(j)
+                if inter[j] == i:
+                    interleave(j, j in ON_S)
+            for j in range(2, n_units):
+                if mul[j] == i:
+                    multiply(j)

@@ -18,10 +18,10 @@ FLOPS = 4 * 2 * 512 * 1024 * 1024
 
 P = 128
 HALF = 256
-ON_S = (9,)
-ON_V = (15,)
-LAG = {3: 1, 7: 1, 14: 1, 15: 1}
-SX = {}
+ON_S = (3, 7, 11)
+LAST = 15
+LAG = {}
+SX = {9: 1, 11: 1, 13: 1}
 IX = {13: 1}
 
 
@@ -37,103 +37,121 @@ def tile_ssystemlogheunslope_x2_kernel(
         psum_t = ctx.enter_context(tc.psum_pool(name="psum_t", bufs=2))
         ctx.enter_context(tc.manual_schedule())
 
-        vec = keep.tile([P, 3, 4, 4], BF16, name="vec")
-        for a, v in enumerate((s, la, lb)):
-            nc.scalar.dma_start(out=vec[:, a, 0:2], in_=v.rearrange("(g p t) -> p g t", p=P, t=4))
-        scale_raw = keep.tile([P, 4, 1024], U8, name="scale_raw", align_bytes=64)
-        nc.vector.memset(scale_raw[:, 0:2].rearrange("p a n -> p (a n)").bitcast(I32), 0)
-        nc.vector.memset(scale_raw[:, 2:4].rearrange("p a n -> p (a n)").bitcast(I32), 0)
-        ident = keep.tile([P, P], F32, name="ident")
-        make_identity(nc, ident[:])
-        y_tok = [keep.tile([P, 1024], BF16, name="y_tok%d" % r) for r in range(4)]
-        word_raw = [keep.tile([P, 2, 2048], U8, name="word_raw%d" % w, align_bytes=64) for w in range(2)]
-        def load_words(grp):
-            for w, words in enumerate((g_words, h_words)):
-                nc.sync.dma_start(
-                    out=word_raw[w][:, :, 1024 * grp : 1024 * (grp + 1)].bitcast(I32),
-                    in_=words[:, :, 1024 * grp : 1024 * (grp + 1)].rearrange("k p b -> p k b").bitcast(I32),
-                )
-
-        for r in range(2):
-            nc.sync.dma_start(out=y_tok[r][:], in_=y[P * r : P * (r + 1), :])
-        load_words(0)
         warm = keep.tile([P, 1], F32, name="warm")
-        for w, sc in enumerate((g_scales, h_scales)):
+        vec = keep.tile([P, 3, 4, 4], BF16, name="vec")
+        scale_raw = keep.tile([P, 4, 1024], U8, name="scale_raw", align_bytes=64)
+        word_raw = [keep.tile([P, 2, 2048], U8, name="word_raw%d" % w, align_bytes=64) for w in range(2)]
+        ident = keep.tile([P, P], F32, name="ident")
+        y_tok = [keep.tile([P, 2, 1024], BF16, name="y_tok%d" % h) for h in range(2)]
+
+        def load_y(half, grp):
+            cols = slice(512 * grp, 512 * (grp + 1))
+            nc.sync.dma_start(
+                out=y_tok[half][:, :, cols], in_=y[HALF * half : HALF * (half + 1), cols].rearrange("(r p) k -> p r k", p=P)
+            )
+
+        def load_words(w, grp):
+            words = (g_words, h_words)[w]
+            nc.sync.dma_start(
+                out=word_raw[w][:, :, 1024 * grp : 1024 * (grp + 1)].bitcast(I32),
+                in_=words[:, :, 1024 * grp : 1024 * (grp + 1)].rearrange("k p b -> p k b").bitcast(I32),
+            )
+
+        def load_scales(w):
+            sc = (g_scales, h_scales)[w]
             for q in range(4):
-                nc.scalar.dma_start(
+                nc.sync.dma_start(
                     out=scale_raw[32 * q : 32 * q + 4, 2 * w : 2 * w + 2, :].bitcast(I32),
                     in_=sc[:, 4 * q : 4 * q + 4, :].rearrange("k r n -> r k n").bitcast(I32),
                 )
+
+        def load_vector(a):
+            nc.gpsimd.dma_start(out=vec[:, a, 0:2], in_=(s, la, lb)[a].rearrange("(g p t) -> p g t", p=P, t=4))
+
         nc.vector.memset(warm[:], 0.0)
         nc.scalar.activation(warm[:], warm[:], ACT.Exp)
-        for r in range(2, 4):
-            nc.sync.dma_start(out=y_tok[r][:], in_=y[P * r : P * (r + 1), :])
-        load_words(1)
+        load_vector(0)
+        make_identity(nc, ident[:])
+        load_vector(1)
+        load_vector(2)
+        for w in range(2):
+            nc.vector.memset(scale_raw[:, 2 * w : 2 * w + 2].rearrange("p a n -> p (a n)").bitcast(I32), 0)
+        load_words(0, 0)
+        load_y(0, 0)
+        load_y(0, 1)
+        load_words(1, 0)
+        load_scales(0)
+        load_scales(1)
+        for grp in range(2):
+            load_y(1, grp)
+        load_words(0, 1)
+        load_words(1, 1)
 
         vec_f = keep.tile([P, 3, 8], F32, name="vec_f")
         words_p = [keep.tile([P, 2, 8, 256], U8, name="words_p%d" % w, align_bytes=64) for w in range(2)]
         scale_p = keep.tile([P, 4, 8, P], U8, name="scale_p", align_bytes=64)
         y4 = keep.tile([P, 2, 512, 4], BF16, name="y4", align_bytes=64)
-        codes = [keep.tile([P, 2, 512], U32, name="codes%d" % i, align_bytes=64) for i in range(2)]
-        scales = [keep.tile([P, 2, 512], U8, name="scales%d" % i, align_bytes=64) for i in range(2)]
+        codes = [keep.tile([P, 2, 2, HALF], U32, name="codes%d" % i, align_bytes=64) for i in range(2)]
+        scales = [keep.tile([P, 2, 2, HALF], U8, name="scales%d" % i, align_bytes=64) for i in range(2)]
+        out_sc = keep.tile([P, 2, 512], U8, name="out_sc", align_bytes=64)
         k1h = keep.tile([P, 8, 512], F32, name="k1h", align_bytes=64)
         y1 = keep.tile([P, 8, 512], F32, name="y1", align_bytes=64)
 
         live = {}
 
         def vectors():
-            nc.vector.tensor_copy(out=vec_f[:, 0], in_=vec[:, 0, 0:2].rearrange("p g t -> p (g t)"))
             nc.vector.tensor_scalar_add(vec_f[:, 1:3], vec[:, 1:3, 0:2].rearrange("p a g t -> p a (g t)"), math.log(0.5))
+            nc.vector.tensor_copy(out=vec_f[:, 0], in_=vec[:, 0, 0:2].rearrange("p g t -> p (g t)"))
 
         def quantize(stage, grp, t0, src):
             nc.vector.quantize_mx(
-                out=codes[stage][:, grp, t0 : t0 + HALF].bitcast(FP8X4),
-                scales=scales[stage][:, grp, t0 : t0 + HALF],
+                out=codes[stage][:, t0 // HALF, grp, :].bitcast(FP8X4),
+                scales=scales[stage][:, t0 // HALF, grp, :],
                 in_=src[:].rearrange("p n t -> p (n t)"),
             )
 
         def head_t(half, grp):
             bank = psum_t.tile([P, 2, HALF], F32, name="bank", tag="tr")
             for r in range(2):
-                yw = y_tok[2 * half + r][:].bitcast(F32)
+                yw = y_tok[half][:, r, :].bitcast(F32)
                 for u in range(2):
                     nc.tensor.transpose(
                         bank[:, u, P * r : P * (r + 1)], yw[:, 256 * grp + u : 256 * (grp + 1) : 2], ident[:]
                     )
             t0 = HALF * half
-            u0 = work.tile([P, HALF, 4], BF16, name="u0", tag="u_i", align_bytes=64)
+            if grp == 0:
+                live["u0", half] = work.tile([P, 2, HALF, 4], BF16, name="u0", tag="u0", align_bytes=64)
             nc.vector.tensor_tensor(
-                out=u0[:].rearrange("p n (u e) -> p n u e", e=2),
+                out=live["u0", half][:, grp].rearrange("p n (u e) -> p n u e", e=2),
                 in0=bank[:].bitcast(BF16).rearrange("p u (n e) -> p n u e", e=2),
                 in1=vec[:, 0, grp, :].rearrange("p (u e) -> p u e", e=2).unsqueeze(1).to_broadcast([P, HALF, 2, 2]),
                 op=ALU.mult,
             )
-            live["u0", half, grp] = u0
             nc.scalar.copy(
                 out=y4[:, grp, t0 : t0 + HALF, :].rearrange("p n t -> p (n t)").bitcast(F32).rearrange("p (n u) -> p n u", u=2),
                 in_=bank[:].rearrange("p u n -> p n u"),
             )
 
-        def head_q(half, grp):
-            quantize(0, grp, HALF * half, live["u0", half, grp])
+        def head_q(half):
+            nc.vector.quantize_mx(
+                out=codes[0][:, half].rearrange("p g n -> p (g n)").bitcast(FP8X4),
+                scales=scales[0][:, half].rearrange("p g n -> p (g n)"),
+                in_=live["u0", half][:].rearrange("p g n t -> p (g n t)"),
+            )
 
-        def permute_words(slot):
-            g, t = slot // 4, slot % 4
-            for w in range(2):
-                src = word_raw[w][:].rearrange("p k (g m t b) -> p k g m t b", g=2, t=4, b=2)
-                nc.vector.tensor_copy(
-                    out=words_p[w][:, :, slot, :].rearrange("p k (m b) -> p k m b", b=2), in_=src[:, :, g, :, t, :]
-                )
+        def permute_words(w, pr):
+            a = 2 * (pr % 2)
+            src = word_raw[w][:].rearrange("p k (g m t b) -> p k g t m b", g=2, t=4, b=2)
+            nc.vector.tensor_copy(
+                out=words_p[w][:, :, 2 * pr : 2 * pr + 2, :].rearrange("p k t (m b) -> p k t m b", b=2),
+                in_=src[:, :, pr // 2, a : a + 2],
+            )
 
         def permute_scales(w, g):
             src = scale_raw[:].rearrange("p a (g m t) -> p a g t m", g=2, t=4)
             nc.vector.tensor_copy(
                 out=scale_p[:, 2 * w : 2 * w + 2, 4 * g : 4 * g + 4, :], in_=src[:, 2 * w : 2 * w + 2, g]
             )
-
-        def permute_pair(pr):
-            permute_words(2 * pr)
-            permute_words(2 * pr + 1)
 
         units = [(st, pr, hf) for st in range(2) for hf in range(2) for pr in range(4)]
         n_units = len(units)
@@ -146,14 +164,14 @@ def tile_ssystemlogheunslope_x2_kernel(
                 for j in range(2):
                     slot = 2 * pr + j
                     for q in range(2):
-                        c0 = HALF * hf + P * q
+                        c0 = P * q
                         for k in range(2):
                             nc.tensor.matmul_mx(
                                 out=ps[:, j, P * q : P * (q + 1)],
                                 lhsT=words_p[w][:, k, slot, :].bitcast(FP4X4),
                                 lhsT_scale=scale_p[:, 2 * w + k, slot, :],
-                                rhs=codes[st][:, k, c0 : c0 + P].bitcast(FP8X4),
-                                rhs_scale=scales[st][:, k, c0 : c0 + P],
+                                rhs=codes[st][:, hf, k, c0 : c0 + P].bitcast(FP8X4),
+                                rhs_scale=scales[st][:, hf, k, c0 : c0 + P],
                                 start=(k == 0),
                                 stop=(k == 1),
                             )
@@ -218,6 +236,19 @@ def tile_ssystemlogheunslope_x2_kernel(
                     out=live["o", hf, grp][:, a : a + 2, :], in0=live[i]["tt"][:], in1=live[i]["ex"][:, 1], op=ALU.subtract
                 )
 
+        def finish_last():
+            hf, grp = 1, 1
+            ex = live[LAST]["ex"]
+            o = live["o", hf, grp]
+            tt = work.tile([P, 2, HALF], F32, name="tt", tag="tt")
+            halves = [slice(P * r, P * (r + 1)) for r in range(2)]
+            for n in halves:
+                nc.vector.tensor_tensor(
+                    out=tt[:, :, n], in0=k1h[:, 6:8, HALF + n.start : HALF + n.stop], in1=ex[:, 0, :, n], op=ALU.add
+                )
+            for n in halves:
+                nc.vector.tensor_tensor(out=o[:, 2:4, n], in0=tt[:, :, n], in1=ex[:, 1, :, n], op=ALU.subtract)
+
         def finish_s(i):
             st, pr, hf = units[i]
             t0 = HALF * hf
@@ -243,7 +274,7 @@ def tile_ssystemlogheunslope_x2_kernel(
                     nc.scalar.copy(out=orow[:], in_=bank[:].rearrange("p t m -> p m t"))
                     r0 = t0 + P * r
                     c0 = 512 * grp
-                    (nc.scalar if i == 15 else nc.sync).dma_start(out=out_0[r0 : r0 + P, c0 : c0 + 512], in_=orow[:].rearrange("p m t -> p (m t)"))
+                    (nc.scalar if i == LAST and r == 1 else nc.sync).dma_start(out=out_0[r0 : r0 + P, c0 : c0 + 512], in_=orow[:].rearrange("p m t -> p (m t)"))
 
         def interleave(i, on_scalar):
             st, pr, hf = units[i]
@@ -271,21 +302,22 @@ def tile_ssystemlogheunslope_x2_kernel(
                 quantize(1, grp, t0, ui)
                 return
             oc = work.tile([P, HALF], U32, name="oc", tag="oc", align_bytes=64)
-            osc = work.tile([P, HALF], U8, name="osc", tag="osc", align_bytes=64)
-            nc.vector.quantize_mx(out=oc[:].bitcast(FP8X4), scales=osc[:], in_=ui[:].rearrange("p n t -> p (n t)"))
+            nc.vector.quantize_mx(
+                out=oc[:].bitcast(FP8X4), scales=out_sc[:, grp, t0 : t0 + HALF], in_=ui[:].rearrange("p n t -> p (n t)")
+            )
             nc.sync.dma_start(out=out_words[grp][:, 4 * t0 : 4 * (t0 + HALF)].bitcast(I32), in_=oc[:].bitcast(I32))
-            for q in range(4):
-                nc.sync.dma_start(
-                    out=out_2[grp, 4 * q : 4 * q + 4, t0 : t0 + HALF].bitcast(I32),
-                    in_=osc[32 * q : 32 * q + 4, :].bitcast(I32),
-                )
+            if i == LAST:
+                for q in range(4):
+                    nc.sync.dma_start(
+                        out=out_2[:, 4 * q : 4 * q + 4, :].rearrange("g r n -> r g n").bitcast(I32),
+                        in_=out_sc[32 * q : 32 * q + 4, :, :].bitcast(I32),
+                    )
 
-        permute_scales(0, 0)
-        vectors()
+        permute_words(0, 0)
         for grp in range(2):
             head_t(0, grp)
-        for grp in range(2):
-            head_q(0, grp)
+        permute_words(0, 1)
+        head_q(0)
         fin = [i + LAG.get(i, 2) for i in range(n_units)]
         fin_s = [fin[i] + SX.get(i, 0) for i in range(n_units)]
         inter = {i: fin[i] + (0 if i in ON_S else 1) + IX.get(i, 0) for i in range(1, n_units, 2)}
@@ -293,33 +325,36 @@ def tile_ssystemlogheunslope_x2_kernel(
         mul = [i - 2 for i in range(n_units)]
         for i in range(8, n_units):
             mul[i] = max(i - 2, max(quant[j] for j in ((1, 3) if i < 12 else (5, 7))))
+        permute_scales(0, 0)
+        permute_words(1, 0)
         permute_scales(1, 0)
-        permute_pair(0)
+        vectors()
         multiply(0)
-        permute_pair(1)
+        permute_words(1, 1)
         multiply(1)
         for i in range(n_units + 5):
             if i < n_units:
                 subtract_y(i)
                 exps(i)
-                if i not in ON_V:
+                if i != LAST:
                     difference(i, nc.gpsimd)
             if i == 0:
                 for w in range(2):
                     permute_scales(w, 1)
-                permute_pair(2)
+                    permute_words(w, 2)
             if i == 1:
-                permute_pair(3)
+                for w in range(2):
+                    permute_words(w, 3)
                 for grp in range(2):
                     head_t(1, grp)
             if i == 2:
-                for grp in range(2):
-                    head_q(1, grp)
+                head_q(1)
             for j in range(n_units):
                 if fin[j] == i:
-                    if j in ON_V:
-                        difference(j, nc.vector)
-                    finish_v(j)
+                    if j == LAST:
+                        finish_last()
+                    else:
+                        finish_v(j)
                 if fin_s[j] == i:
                     finish_s(j)
             for j in inter:

@@ -20,7 +20,9 @@ P = 128
 HALF = 256
 ON_S = (3, 7, 11)
 LAST = 15
-LAG = {}
+ON_V = (0,)
+HEAD = 0
+LAG = {0: 1, 3: 1, 9: 1}
 SX = {9: 1, 11: 1, 13: 1}
 IX = {13: 1}
 
@@ -33,27 +35,41 @@ def tile_ssystemlogheunslope_x2_kernel(
     with ExitStack() as ctx:
         keep = ctx.enter_context(tc.tile_pool(name="keep", bufs=1))
         work = ctx.enter_context(tc.tile_pool(name="work", bufs=3))
-        psum = ctx.enter_context(tc.psum_pool(name="psum", bufs=3))
-        psum_t = ctx.enter_context(tc.psum_pool(name="psum_t", bufs=2))
+        psum = ctx.enter_context(tc.psum_pool(name="psum", bufs=2))
+        psum_t = ctx.enter_context(tc.psum_pool(name="psum_t", bufs=4))
         ctx.enter_context(tc.manual_schedule())
 
-        warm = keep.tile([P, 1], F32, name="warm")
-        vec = keep.tile([P, 3, 4, 4], BF16, name="vec")
-        scale_raw = keep.tile([P, 4, 1024], U8, name="scale_raw", align_bytes=64)
-        word_raw = [keep.tile([P, 2, 2048], U8, name="word_raw%d" % w, align_bytes=64) for w in range(2)]
-        ident = keep.tile([P, P], F32, name="ident")
-        y_tok = [keep.tile([P, 2, 1024], BF16, name="y_tok%d" % h) for h in range(2)]
+        def grid(name, shape, dtype, *dims):
+            if not dims:
+                return keep.tile(shape, dtype, name=name, align_bytes=64)
+            return [grid("%s_%d" % (name, i), shape, dtype, *dims[1:]) for i in range(dims[0])]
+
+        warm = grid("warm", [P, 1], F32)
+        vec = grid("vec", [P, 4, 4], BF16, 3)
+        vec_f = grid("vec_f", [P, 8], F32, 3)
+        ident = grid("ident", [P, P], F32)
+        y_tok = grid("y_tok", [P, 2, 512], BF16, 2, 2)
+        y4 = grid("y4", [P, HALF, 4], BF16, 2, 2)
+        word_raw = grid("word_raw", [P, 2, 1024], U8, 2, 2)
+        words_p = grid("words_p", [P, 2, 2, 256], U8, 2, 4)
+        scale_raw = grid("scale_raw", [P, 2, 1024], U8, 2)
+        scale_p = grid("scale_p", [P, 2, 4, P], U8, 2, 2)
+        codes = grid("codes", [P, 2, HALF], U32, 2, 2)
+        scales = grid("scales", [P, 2, HALF], U8, 2, 2)
+        k1h = grid("k1h", [P, 2, HALF], F32, 2, 4)
+        y1 = grid("y1", [P, 2, HALF], F32, 2, 4)
+        out_sc = grid("out_sc", [P, 2, 512], U8)
 
         def load_y(half, grp):
-            cols = slice(512 * grp, 512 * (grp + 1))
             nc.sync.dma_start(
-                out=y_tok[half][:, :, cols], in_=y[HALF * half : HALF * (half + 1), cols].rearrange("(r p) k -> p r k", p=P)
+                out=y_tok[half][grp][:],
+                in_=y[HALF * half : HALF * (half + 1), 512 * grp : 512 * (grp + 1)].rearrange("(r p) k -> p r k", p=P),
             )
 
         def load_words(w, grp):
             words = (g_words, h_words)[w]
             nc.sync.dma_start(
-                out=word_raw[w][:, :, 1024 * grp : 1024 * (grp + 1)].bitcast(I32),
+                out=word_raw[w][grp][:].bitcast(I32),
                 in_=words[:, :, 1024 * grp : 1024 * (grp + 1)].rearrange("k p b -> p k b").bitcast(I32),
             )
 
@@ -61,21 +77,21 @@ def tile_ssystemlogheunslope_x2_kernel(
             sc = (g_scales, h_scales)[w]
             for q in range(4):
                 nc.sync.dma_start(
-                    out=scale_raw[32 * q : 32 * q + 4, 2 * w : 2 * w + 2, :].bitcast(I32),
+                    out=scale_raw[w][32 * q : 32 * q + 4, :, :].bitcast(I32),
                     in_=sc[:, 4 * q : 4 * q + 4, :].rearrange("k r n -> r k n").bitcast(I32),
                 )
 
         def load_vector(a):
-            nc.gpsimd.dma_start(out=vec[:, a, 0:2], in_=(s, la, lb)[a].rearrange("(g p t) -> p g t", p=P, t=4))
+            nc.gpsimd.dma_start(out=vec[a][:, 0:2], in_=(s, la, lb)[a].rearrange("(g p t) -> p g t", p=P, t=4))
 
-        nc.vector.memset(warm[:], 0.0)
-        nc.scalar.activation(warm[:], warm[:], ACT.Exp)
         load_vector(0)
         make_identity(nc, ident[:])
         load_vector(1)
         load_vector(2)
         for w in range(2):
-            nc.vector.memset(scale_raw[:, 2 * w : 2 * w + 2].rearrange("p a n -> p (a n)").bitcast(I32), 0)
+            nc.vector.memset(scale_raw[w][:].rearrange("p a n -> p (a n)").bitcast(I32), 0)
+        nc.vector.memset(warm[:], 0.0)
+        nc.scalar.activation(warm[:], warm[:], ACT.Exp)
         load_words(0, 0)
         load_y(0, 0)
         load_y(0, 1)
@@ -84,74 +100,52 @@ def tile_ssystemlogheunslope_x2_kernel(
         load_scales(1)
         for grp in range(2):
             load_y(1, grp)
-        load_words(0, 1)
-        load_words(1, 1)
-
-        vec_f = keep.tile([P, 3, 8], F32, name="vec_f")
-        words_p = [keep.tile([P, 2, 8, 256], U8, name="words_p%d" % w, align_bytes=64) for w in range(2)]
-        scale_p = keep.tile([P, 4, 8, P], U8, name="scale_p", align_bytes=64)
-        y4 = keep.tile([P, 2, 512, 4], BF16, name="y4", align_bytes=64)
-        codes = [keep.tile([P, 2, 2, HALF], U32, name="codes%d" % i, align_bytes=64) for i in range(2)]
-        scales = [keep.tile([P, 2, 2, HALF], U8, name="scales%d" % i, align_bytes=64) for i in range(2)]
-        out_sc = keep.tile([P, 2, 512], U8, name="out_sc", align_bytes=64)
-        k1h = keep.tile([P, 8, 512], F32, name="k1h", align_bytes=64)
-        y1 = keep.tile([P, 8, 512], F32, name="y1", align_bytes=64)
+        for w in range(2):
+            load_words(w, 1)
 
         live = {}
 
         def vectors():
-            nc.vector.tensor_scalar_add(vec_f[:, 1:3], vec[:, 1:3, 0:2].rearrange("p a g t -> p a (g t)"), math.log(0.5))
-            nc.vector.tensor_copy(out=vec_f[:, 0], in_=vec[:, 0, 0:2].rearrange("p g t -> p (g t)"))
-
-        def quantize(stage, grp, t0, src):
-            nc.vector.quantize_mx(
-                out=codes[stage][:, t0 // HALF, grp, :].bitcast(FP8X4),
-                scales=scales[stage][:, t0 // HALF, grp, :],
-                in_=src[:].rearrange("p n t -> p (n t)"),
-            )
+            for a in (1, 2):
+                nc.vector.tensor_scalar_add(vec_f[a][:], vec[a][:, 0:2].rearrange("p g t -> p (g t)"), math.log(0.5))
+            nc.vector.tensor_copy(out=vec_f[0][:], in_=vec[0][:, 0:2].rearrange("p g t -> p (g t)"))
 
         def head_t(half, grp):
             bank = psum_t.tile([P, 2, HALF], F32, name="bank", tag="tr")
             for r in range(2):
-                yw = y_tok[half][:, r, :].bitcast(F32)
+                yw = y_tok[half][grp][:, r, :].bitcast(F32)
                 for u in range(2):
-                    nc.tensor.transpose(
-                        bank[:, u, P * r : P * (r + 1)], yw[:, 256 * grp + u : 256 * (grp + 1) : 2], ident[:]
-                    )
-            t0 = HALF * half
+                    nc.tensor.transpose(bank[:, u, P * r : P * (r + 1)], yw[:, u : 256 : 2], ident[:])
+            live["yb", half, grp] = bank
             if grp == 0:
                 live["u0", half] = work.tile([P, 2, HALF, 4], BF16, name="u0", tag="u0", align_bytes=64)
             nc.vector.tensor_tensor(
                 out=live["u0", half][:, grp].rearrange("p n (u e) -> p n u e", e=2),
                 in0=bank[:].bitcast(BF16).rearrange("p u (n e) -> p n u e", e=2),
-                in1=vec[:, 0, grp, :].rearrange("p (u e) -> p u e", e=2).unsqueeze(1).to_broadcast([P, HALF, 2, 2]),
+                in1=vec[0][:, grp, :].rearrange("p (u e) -> p u e", e=2).unsqueeze(1).to_broadcast([P, HALF, 2, 2]),
                 op=ALU.mult,
             )
             nc.scalar.copy(
-                out=y4[:, grp, t0 : t0 + HALF, :].rearrange("p n t -> p (n t)").bitcast(F32).rearrange("p (n u) -> p n u", u=2),
+                out=y4[half][grp][:].rearrange("p n t -> p (n t)").bitcast(F32).rearrange("p (n u) -> p n u", u=2),
                 in_=bank[:].rearrange("p u n -> p n u"),
             )
 
         def head_q(half):
             nc.vector.quantize_mx(
-                out=codes[0][:, half].rearrange("p g n -> p (g n)").bitcast(FP8X4),
-                scales=scales[0][:, half].rearrange("p g n -> p (g n)"),
+                out=codes[0][half][:].rearrange("p g n -> p (g n)").bitcast(FP8X4),
+                scales=scales[0][half][:].rearrange("p g n -> p (g n)"),
                 in_=live["u0", half][:].rearrange("p g n t -> p (g n t)"),
             )
 
         def permute_words(w, pr):
-            a = 2 * (pr % 2)
-            src = word_raw[w][:].rearrange("p k (g m t b) -> p k g t m b", g=2, t=4, b=2)
+            src = word_raw[w][pr // 2][:].rearrange("p k (m t b) -> p k t m b", t=4, b=2)
             nc.vector.tensor_copy(
-                out=words_p[w][:, :, 2 * pr : 2 * pr + 2, :].rearrange("p k t (m b) -> p k t m b", b=2),
-                in_=src[:, :, pr // 2, a : a + 2],
+                out=words_p[w][pr][:].rearrange("p k t (m b) -> p k t m b", b=2), in_=src[:, :, pr % 2 : 4 : 2]
             )
 
         def permute_scales(w, g):
-            src = scale_raw[:].rearrange("p a (g m t) -> p a g t m", g=2, t=4)
-            nc.vector.tensor_copy(
-                out=scale_p[:, 2 * w : 2 * w + 2, 4 * g : 4 * g + 4, :], in_=src[:, 2 * w : 2 * w + 2, g]
-            )
+            src = scale_raw[w][:].rearrange("p a (g m t) -> p a g t m", g=2, t=4)
+            nc.vector.tensor_copy(out=scale_p[w][g][:], in_=src[:, :, g])
 
         units = [(st, pr, hf) for st in range(2) for hf in range(2) for pr in range(4)]
         n_units = len(units)
@@ -162,149 +156,137 @@ def tile_ssystemlogheunslope_x2_kernel(
             for w in range(2):
                 ps = psum.tile([P, 2, HALF], F32, name="ps%d" % w, tag="ps%d" % w)
                 for j in range(2):
-                    slot = 2 * pr + j
+                    t = pr % 2 + 2 * j
                     for q in range(2):
-                        c0 = P * q
+                        cols = slice(P * q, P * (q + 1))
                         for k in range(2):
                             nc.tensor.matmul_mx(
-                                out=ps[:, j, P * q : P * (q + 1)],
-                                lhsT=words_p[w][:, k, slot, :].bitcast(FP4X4),
-                                lhsT_scale=scale_p[:, 2 * w + k, slot, :],
-                                rhs=codes[st][:, hf, k, c0 : c0 + P].bitcast(FP8X4),
-                                rhs_scale=scales[st][:, hf, k, c0 : c0 + P],
+                                out=ps[:, j, cols],
+                                lhsT=words_p[w][pr][:, k, j, :].bitcast(FP4X4),
+                                lhsT_scale=scale_p[w][pr // 2][:, k, t, :],
+                                rhs=codes[st][hf][:, k, cols].bitcast(FP8X4),
+                                rhs_scale=scales[st][hf][:, k, cols],
                                 start=(k == 0),
                                 stop=(k == 1),
                             )
                 banks.append(ps)
-            live[i] = {"ps": banks}
+            live["ps", i] = banks
 
         def y_view(i):
             st, pr, hf = units[i]
-            t0 = HALF * hf
             if st == 0:
-                a = 2 * (pr % 2)
-                return y4[:, pr // 2, t0 : t0 + HALF, a : a + 2].rearrange("p n t -> p t n")
-            return y1[:, 2 * pr : 2 * pr + 2, t0 : t0 + HALF]
+                return y4[hf][pr // 2][:, :, pr % 2 : 4 : 2].rearrange("p n t -> p t n")
+            return y1[hf][pr][:]
+
+        def y_psum(i):
+            st, pr, hf = units[i]
+            return live["yb", hf, pr // 2][:].bitcast(BF16).rearrange("p u (n e) -> p e u n", e=2)[:, pr % 2]
 
         def subtract_y(i):
             ar = work.tile([P, 2, 2, HALF], F32, name="ar", tag="ar")
             for w in range(2):
-                nc.vector.tensor_tensor(out=ar[:, w], in0=live[i]["ps"][w][:], in1=y_view(i), op=ALU.subtract)
-            live[i]["ar"] = ar
+                nc.vector.tensor_tensor(out=ar[:, w], in0=live["ps", i][w][:], in1=y_view(i), op=ALU.subtract)
+            live["ar", i] = ar
 
         def exps(i):
             st, pr, hf = units[i]
             ex = work.tile([P, 2, 2, HALF], F32, name="ex", tag="ex")
             for w in range(2):
                 for j in range(2):
-                    slot = 2 * pr + j
+                    slot = 4 * (pr // 2) + pr % 2 + 2 * j
                     nc.scalar.activation(
-                        ex[:, w, j], live[i]["ar"][:, w, j], ACT.Exp, bias=vec_f[:, 1 + w, slot : slot + 1]
+                        ex[:, w, j], live["ar", i][:, w, j], ACT.Exp, bias=vec_f[1 + w][:, slot : slot + 1]
                     )
-            live[i]["ex"] = ex
+            live["ex", i] = ex
 
         def difference(i, eng):
             st, pr, hf = units[i]
-            t0 = HALF * hf
-            k_view = k1h[:, 2 * pr : 2 * pr + 2, t0 : t0 + HALF]
-            ex = live[i]["ex"]
+            ex = live["ex", i]
             if st == 0:
-                eng.tensor_tensor(out=k_view, in0=ex[:, 0], in1=ex[:, 1], op=ALU.subtract)
+                eng.tensor_tensor(out=k1h[hf][pr][:], in0=ex[:, 0], in1=ex[:, 1], op=ALU.subtract)
             else:
                 tt = work.tile([P, 2, HALF], F32, name="tt", tag="tt")
-                eng.tensor_tensor(out=tt[:], in0=k_view, in1=ex[:, 0], op=ALU.add)
-                live[i]["tt"] = tt
+                eng.tensor_tensor(out=tt[:], in0=k1h[hf][pr][:], in1=ex[:, 0], op=ALU.add)
+                live["tt", i] = tt
 
         def finish_v(i):
             st, pr, hf = units[i]
-            t0 = HALF * hf
             grp = pr // 2
             if st == 0:
                 nc.vector.scalar_tensor_tensor(
-                    out=y1[:, 2 * pr : 2 * pr + 2, t0 : t0 + HALF],
-                    in0=k1h[:, 2 * pr : 2 * pr + 2, t0 : t0 + HALF],
-                    scalar=0.4,
-                    in1=y_view(i),
-                    op0=ALU.mult,
-                    op1=ALU.add,
+                    out=y1[hf][pr][:], in0=k1h[hf][pr][:], scalar=0.4, in1=y_psum(i), op0=ALU.mult, op1=ALU.add
                 )
-            else:
-                if pr % 2 == 0:
-                    live["o", hf, grp] = work.tile([P, 4, HALF], F32, name="o", tag="o")
-                a = 2 * (pr % 2)
-                nc.vector.tensor_tensor(
-                    out=live["o", hf, grp][:, a : a + 2, :], in0=live[i]["tt"][:], in1=live[i]["ex"][:, 1], op=ALU.subtract
-                )
-
-        def finish_last():
-            hf, grp = 1, 1
-            ex = live[LAST]["ex"]
+                return
+            if pr % 2 == 0:
+                live["o", hf, grp] = work.tile([P, 2, 4, P], F32, name="o", tag="o")
             o = live["o", hf, grp]
-            tt = work.tile([P, 2, HALF], F32, name="tt", tag="tt")
-            halves = [slice(P * r, P * (r + 1)) for r in range(2)]
-            for n in halves:
+            if i != LAST:
                 nc.vector.tensor_tensor(
-                    out=tt[:, :, n], in0=k1h[:, 6:8, HALF + n.start : HALF + n.stop], in1=ex[:, 0, :, n], op=ALU.add
+                    out=o[:, :, pr % 2 : 4 : 2, :],
+                    in0=live["tt", i][:].rearrange("p j (r n) -> p r j n", r=2),
+                    in1=live["ex", i][:, 1].rearrange("p j (r n) -> p r j n", r=2),
+                    op=ALU.subtract,
                 )
-            for n in halves:
-                nc.vector.tensor_tensor(out=o[:, 2:4, n], in0=tt[:, :, n], in1=ex[:, 1, :, n], op=ALU.subtract)
+                return
+            tt = work.tile([P, 2, 2, P], F32, name="tl", tag="tt")
+            ex = live["ex", i][:].rearrange("p w j (r n) -> p w r j n", r=2)
+            kk = k1h[hf][pr][:].rearrange("p j (r n) -> p r j n", r=2)
+            for r in range(2):
+                nc.vector.tensor_tensor(out=tt[:, r], in0=kk[:, r], in1=ex[:, 0, r], op=ALU.add)
+            for r in range(2):
+                nc.vector.tensor_tensor(out=o[:, r, pr % 2 : 4 : 2, :], in0=tt[:, r], in1=ex[:, 1, r], op=ALU.subtract)
 
         def finish_s(i):
             st, pr, hf = units[i]
-            t0 = HALF * hf
             grp = pr // 2
             if st == 0:
                 if pr % 2 == 0:
                     live["u1s", hf, grp] = work.tile([P, 2, HALF, 2], BF16, name="u1s", tag="u1s", align_bytes=64)
                 for j in range(2):
-                    slot = 2 * pr + j
+                    slot = 4 * grp + pr % 2 + 2 * j
                     nc.scalar.activation(
-                        live["u1s", hf, grp][:, (slot % 4) // 2, :, slot % 2],
-                        y1[:, slot, t0 : t0 + HALF],
-                        ACT.Copy,
-                        scale=vec_f[:, 0, slot : slot + 1],
+                        live["u1s", hf, grp][:, j, :, pr % 2], y1[hf][pr][:, j, :], ACT.Copy, scale=vec_f[0][:, slot : slot + 1]
                     )
             elif pr % 2 == 1:
                 o = live["o", hf, grp]
                 for r in range(2):
                     bank = psum_t.tile([P, 4, P], F32, name="obank", tag="tr")
                     for t in range(4):
-                        nc.tensor.transpose(bank[:, t, :], o[:, t, P * r : P * (r + 1)], ident[:])
+                        nc.tensor.transpose(bank[:, t, :], o[:, r, t, :], ident[:])
                     orow = work.tile([P, P, 4], F32, name="orow", tag="orow", bufs=6)
                     nc.scalar.copy(out=orow[:], in_=bank[:].rearrange("p t m -> p m t"))
-                    r0 = t0 + P * r
+                    r0 = HALF * hf + P * r
                     c0 = 512 * grp
-                    (nc.scalar if i == LAST and r == 1 else nc.sync).dma_start(out=out_0[r0 : r0 + P, c0 : c0 + 512], in_=orow[:].rearrange("p m t -> p (m t)"))
+                    (nc.scalar if i == LAST and r == 1 else nc.sync).dma_start(
+                        out=out_0[r0 : r0 + P, c0 : c0 + 512], in_=orow[:].rearrange("p m t -> p (m t)")
+                    )
 
         def interleave(i, on_scalar):
             st, pr, hf = units[i]
-            if st == 1:
-                src = live["o", hf, pr // 2][:].rearrange("p t n -> p n t")
             ui = work.tile([P, HALF, 4], BF16, name="ui", tag="u_i", align_bytes=64)
+            copy = nc.scalar.copy if on_scalar else nc.vector.tensor_copy
             if st == 0:
-                pairs = live["u1s", hf, pr // 2][:].rearrange("p u n e -> p u (n e)").bitcast(F32)
-                (nc.scalar.copy if on_scalar else nc.vector.tensor_copy)(
+                copy(
                     out=ui[:].rearrange("p n t -> p (n t)").bitcast(F32).rearrange("p (n u) -> p n u", u=2),
-                    in_=pairs.rearrange("p u n -> p n u"),
+                    in_=live["u1s", hf, pr // 2][:].rearrange("p u n e -> p u (n e)").bitcast(F32).rearrange("p u n -> p n u"),
                 )
-            elif on_scalar:
-                nc.scalar.copy(out=ui[:], in_=src)
             else:
-                nc.vector.tensor_copy(out=ui[:], in_=src)
-            live[i]["ui"] = ui
+                copy(
+                    out=ui[:].rearrange("p (r n) t -> p r n t", r=2),
+                    in_=live["o", hf, pr // 2][:].rearrange("p r t n -> p r n t"),
+                )
+            live["ui", i] = ui
 
         def quantize_unit(i):
             st, pr, hf = units[i]
             t0 = HALF * hf
             grp = pr // 2
-            ui = live[i]["ui"]
+            ui = live["ui", i][:].rearrange("p n t -> p (n t)")
             if st == 0:
-                quantize(1, grp, t0, ui)
+                nc.vector.quantize_mx(out=codes[1][hf][:, grp, :].bitcast(FP8X4), scales=scales[1][hf][:, grp, :], in_=ui)
                 return
             oc = work.tile([P, HALF], U32, name="oc", tag="oc", align_bytes=64)
-            nc.vector.quantize_mx(
-                out=oc[:].bitcast(FP8X4), scales=out_sc[:, grp, t0 : t0 + HALF], in_=ui[:].rearrange("p n t -> p (n t)")
-            )
+            nc.vector.quantize_mx(out=oc[:].bitcast(FP8X4), scales=out_sc[:, grp, t0 : t0 + HALF], in_=ui)
             nc.sync.dma_start(out=out_words[grp][:, 4 * t0 : 4 * (t0 + HALF)].bitcast(I32), in_=oc[:].bitcast(I32))
             if i == LAST:
                 for q in range(4):
@@ -314,9 +296,10 @@ def tile_ssystemlogheunslope_x2_kernel(
                     )
 
         permute_words(0, 0)
+        permute_words(0, 1)
         for grp in range(2):
             head_t(0, grp)
-        permute_words(0, 1)
+        permute_words(1, 0)
         head_q(0)
         fin = [i + LAG.get(i, 2) for i in range(n_units)]
         fin_s = [fin[i] + SX.get(i, 0) for i in range(n_units)]
@@ -326,17 +309,19 @@ def tile_ssystemlogheunslope_x2_kernel(
         for i in range(8, n_units):
             mul[i] = max(i - 2, max(quant[j] for j in ((1, 3) if i < 12 else (5, 7))))
         permute_scales(0, 0)
-        permute_words(1, 0)
+        if HEAD:
+            permute_words(1, 1)
         permute_scales(1, 0)
         vectors()
         multiply(0)
-        permute_words(1, 1)
+        if not HEAD:
+            permute_words(1, 1)
         multiply(1)
-        for i in range(n_units + 5):
+        for i in range(n_units + 9):
             if i < n_units:
                 subtract_y(i)
                 exps(i)
-                if i != LAST:
+                if i != LAST and i not in ON_V:
                     difference(i, nc.gpsimd)
             if i == 0:
                 for w in range(2):
@@ -351,10 +336,9 @@ def tile_ssystemlogheunslope_x2_kernel(
                 head_q(1)
             for j in range(n_units):
                 if fin[j] == i:
-                    if j == LAST:
-                        finish_last()
-                    else:
-                        finish_v(j)
+                    if j in ON_V:
+                        difference(j, nc.vector)
+                    finish_v(j)
                 if fin_s[j] == i:
                     finish_s(j)
             for j in inter:

@@ -18,13 +18,14 @@ FLOPS = 4 * 2 * 512 * 1024 * 1024
 
 P = 128
 HALF = 256
-ON_S = (3, 7, 11)
-LAST = 15
-ON_V = (0,)
-HEAD = 0
-LAG = {0: 1, 3: 1, 9: 1}
-SX = {9: 1, 11: 1, 13: 1}
-IX = {13: 1}
+GROUP = 512
+
+UNITS = [(stage, pair, half) for stage in range(2) for half in range(2) for pair in range(4)]
+LAST = len(UNITS) - 1
+
+FINISH_LAG = {0: 1, 9: 1}
+
+LAID_OUT_BY_SCALAR = (3, 7, 11)
 
 
 def tile_ssystemlogheunslope_x2_kernel(
@@ -32,6 +33,7 @@ def tile_ssystemlogheunslope_x2_kernel(
 ):
     nc = tc.nc
     out_words = out_1.rearrange("g p m t -> g p (m t)")
+
     with ExitStack() as ctx:
         keep = ctx.enter_context(tc.tile_pool(name="keep", bufs=1))
         work = ctx.enter_context(tc.tile_pool(name="work", bufs=3))
@@ -45,307 +47,293 @@ def tile_ssystemlogheunslope_x2_kernel(
             return [grid("%s_%d" % (name, i), shape, dtype, *dims[1:]) for i in range(dims[0])]
 
         warm = grid("warm", [P, 1], F32)
+        ident = grid("ident", [P, P], F32)
         vec = grid("vec", [P, 4, 4], BF16, 3)
         vec_f = grid("vec_f", [P, 8], F32, 3)
-        ident = grid("ident", [P, P], F32)
-        y_tok = grid("y_tok", [P, 2, 512], BF16, 2, 2)
+        y_tok = grid("y_tok", [P, 2, GROUP], BF16, 2, 2)
         y4 = grid("y4", [P, HALF, 4], BF16, 2, 2)
-        word_raw = grid("word_raw", [P, 2, 1024], U8, 2, 2)
-        words_p = grid("words_p", [P, 2, 2, 256], U8, 2, 4)
+        word_raw = grid("word_raw", [P, 2, 2 * GROUP], U8, 2, 2)
+        words = grid("words", [P, 2, 2, 2 * P], U8, 2, 4)
         scale_raw = grid("scale_raw", [P, 2, 1024], U8, 2)
-        scale_p = grid("scale_p", [P, 2, 4, P], U8, 2, 2)
+        scale_w = grid("scale_w", [P, 2, 4, P], U8, 2, 2)
         codes = grid("codes", [P, 2, HALF], U32, 2, 2)
         scales = grid("scales", [P, 2, HALF], U8, 2, 2)
-        k1h = grid("k1h", [P, 2, HALF], F32, 2, 4)
+        k1_half = grid("k1_half", [P, 2, HALF], F32, 2, 4)
         y1 = grid("y1", [P, 2, HALF], F32, 2, 4)
-        out_sc = grid("out_sc", [P, 2, 512], U8)
+        out_scales = grid("out_scales", [P, 2, 512], U8)
+        live = {}
 
         def load_y(half, grp):
             nc.sync.dma_start(
                 out=y_tok[half][grp][:],
-                in_=y[HALF * half : HALF * (half + 1), 512 * grp : 512 * (grp + 1)].rearrange("(r p) k -> p r k", p=P),
+                in_=y[HALF * half : HALF * (half + 1), GROUP * grp : GROUP * (grp + 1)].rearrange("(r p) k -> p r k", p=P),
             )
 
         def load_words(w, grp):
-            words = (g_words, h_words)[w]
             nc.sync.dma_start(
                 out=word_raw[w][grp][:].bitcast(I32),
-                in_=words[:, :, 1024 * grp : 1024 * (grp + 1)].rearrange("k p b -> p k b").bitcast(I32),
+                in_=(g_words, h_words)[w][:, :, 2 * GROUP * grp : 2 * GROUP * (grp + 1)].rearrange("k p b -> p k b").bitcast(I32),
             )
 
         def load_scales(w):
-            sc = (g_scales, h_scales)[w]
             for q in range(4):
                 nc.sync.dma_start(
                     out=scale_raw[w][32 * q : 32 * q + 4, :, :].bitcast(I32),
-                    in_=sc[:, 4 * q : 4 * q + 4, :].rearrange("k r n -> r k n").bitcast(I32),
+                    in_=(g_scales, h_scales)[w][:, 4 * q : 4 * q + 4, :].rearrange("k r n -> r k n").bitcast(I32),
                 )
 
-        def load_vector(a):
-            nc.gpsimd.dma_start(out=vec[a][:, 0:2], in_=(s, la, lb)[a].rearrange("(g p t) -> p g t", p=P, t=4))
-
-        load_vector(0)
-        make_identity(nc, ident[:])
-        load_vector(1)
-        load_vector(2)
-        for w in range(2):
-            nc.vector.memset(scale_raw[w][:].rearrange("p a n -> p (a n)").bitcast(I32), 0)
-        nc.vector.memset(warm[:], 0.0)
-        nc.scalar.activation(warm[:], warm[:], ACT.Exp)
-        load_words(0, 0)
-        load_y(0, 0)
-        load_y(0, 1)
-        load_words(1, 0)
-        load_scales(0)
-        load_scales(1)
-        for grp in range(2):
-            load_y(1, grp)
-        for w in range(2):
-            load_words(w, 1)
-
-        live = {}
+        def load_vector(queue, a):
+            queue.dma_start(out=vec[a][:, 0:2], in_=(s, la, lb)[a].rearrange("(g p t) -> p g t", p=P, t=4))
 
         def vectors():
             for a in (1, 2):
                 nc.vector.tensor_scalar_add(vec_f[a][:], vec[a][:, 0:2].rearrange("p g t -> p (g t)"), math.log(0.5))
             nc.vector.tensor_copy(out=vec_f[0][:], in_=vec[0][:, 0:2].rearrange("p g t -> p (g t)"))
 
-        def head_t(half, grp):
-            bank = psum_t.tile([P, 2, HALF], F32, name="bank", tag="tr")
+        def as_words(tile):
+            return tile.rearrange("p n t -> p (n t)").bitcast(F32).rearrange("p (n u) -> p n u", u=2)
+
+        def transpose_y(half, grp):
+            bank = psum_t.tile([P, 2, HALF], F32, name="y_bank", tag="tr")
             for r in range(2):
-                yw = y_tok[half][grp][:, r, :].bitcast(F32)
+                rows = y_tok[half][grp][:, r, :].bitcast(F32)
                 for u in range(2):
-                    nc.tensor.transpose(bank[:, u, P * r : P * (r + 1)], yw[:, u : 256 : 2], ident[:])
-            live["yb", half, grp] = bank
+                    nc.tensor.transpose(bank[:, u, P * r : P * (r + 1)], rows[:, u : GROUP // 2 : 2], ident[:])
+            live["y_bank", half, grp] = bank
             if grp == 0:
-                live["u0", half] = work.tile([P, 2, HALF, 4], BF16, name="u0", tag="u0", align_bytes=64)
+                live["u", half] = work.tile([P, 2, HALF, 4], BF16, name="u", tag="u", align_bytes=64)
             nc.vector.tensor_tensor(
-                out=live["u0", half][:, grp].rearrange("p n (u e) -> p n u e", e=2),
+                out=live["u", half][:, grp].rearrange("p n (u e) -> p n u e", e=2),
                 in0=bank[:].bitcast(BF16).rearrange("p u (n e) -> p n u e", e=2),
                 in1=vec[0][:, grp, :].rearrange("p (u e) -> p u e", e=2).unsqueeze(1).to_broadcast([P, HALF, 2, 2]),
                 op=ALU.mult,
             )
-            nc.scalar.copy(
-                out=y4[half][grp][:].rearrange("p n t -> p (n t)").bitcast(F32).rearrange("p (n u) -> p n u", u=2),
-                in_=bank[:].rearrange("p u n -> p n u"),
-            )
+            nc.scalar.copy(out=as_words(y4[half][grp][:]), in_=bank[:].rearrange("p u n -> p n u"))
 
-        def head_q(half):
+        def quantize_u(half):
             nc.vector.quantize_mx(
                 out=codes[0][half][:].rearrange("p g n -> p (g n)").bitcast(FP8X4),
                 scales=scales[0][half][:].rearrange("p g n -> p (g n)"),
-                in_=live["u0", half][:].rearrange("p g n t -> p (g n t)"),
+                in_=live["u", half][:].rearrange("p g n t -> p (g n t)"),
             )
 
-        def permute_words(w, pr):
-            src = word_raw[w][pr // 2][:].rearrange("p k (m t b) -> p k t m b", t=4, b=2)
+        def order_words(w, pair):
+            src = word_raw[w][pair // 2][:].rearrange("p k (m t b) -> p k t m b", t=4, b=2)
             nc.vector.tensor_copy(
-                out=words_p[w][pr][:].rearrange("p k t (m b) -> p k t m b", b=2), in_=src[:, :, pr % 2 : 4 : 2]
+                out=words[w][pair][:].rearrange("p k t (m b) -> p k t m b", b=2), in_=src[:, :, pair % 2 : 4 : 2]
             )
 
-        def permute_scales(w, g):
-            src = scale_raw[w][:].rearrange("p a (g m t) -> p a g t m", g=2, t=4)
-            nc.vector.tensor_copy(out=scale_p[w][g][:], in_=src[:, :, g])
-
-        units = [(st, pr, hf) for st in range(2) for hf in range(2) for pr in range(4)]
-        n_units = len(units)
+        def order_scales(w, grp):
+            src = scale_raw[w][:].rearrange("p k (g m t) -> p k g t m", g=2, t=4)
+            nc.vector.tensor_copy(out=scale_w[w][grp][:], in_=src[:, :, grp])
 
         def multiply(i):
-            st, pr, hf = units[i]
+            stage, pair, half = UNITS[i]
             banks = []
             for w in range(2):
-                ps = psum.tile([P, 2, HALF], F32, name="ps%d" % w, tag="ps%d" % w)
+                bank = psum.tile([P, 2, HALF], F32, name="product%d" % w, tag="product%d" % w)
                 for j in range(2):
-                    t = pr % 2 + 2 * j
-                    for q in range(2):
-                        cols = slice(P * q, P * (q + 1))
+                    for r in range(2):
+                        cols = slice(P * r, P * (r + 1))
                         for k in range(2):
                             nc.tensor.matmul_mx(
-                                out=ps[:, j, cols],
-                                lhsT=words_p[w][pr][:, k, j, :].bitcast(FP4X4),
-                                lhsT_scale=scale_p[w][pr // 2][:, k, t, :],
-                                rhs=codes[st][hf][:, k, cols].bitcast(FP8X4),
-                                rhs_scale=scales[st][hf][:, k, cols],
+                                out=bank[:, j, cols],
+                                lhsT=words[w][pair][:, k, j, :].bitcast(FP4X4),
+                                lhsT_scale=scale_w[w][pair // 2][:, k, pair % 2 + 2 * j, :],
+                                rhs=codes[stage][half][:, k, cols].bitcast(FP8X4),
+                                rhs_scale=scales[stage][half][:, k, cols],
                                 start=(k == 0),
                                 stop=(k == 1),
                             )
-                banks.append(ps)
-            live["ps", i] = banks
+                banks.append(bank)
+            live["products", i] = banks
 
-        def y_view(i):
-            st, pr, hf = units[i]
-            if st == 0:
-                return y4[hf][pr // 2][:, :, pr % 2 : 4 : 2].rearrange("p n t -> p t n")
-            return y1[hf][pr][:]
-
-        def y_psum(i):
-            st, pr, hf = units[i]
-            return live["yb", hf, pr // 2][:].bitcast(BF16).rearrange("p u (n e) -> p e u n", e=2)[:, pr % 2]
-
-        def subtract_y(i):
-            ar = work.tile([P, 2, 2, HALF], F32, name="ar", tag="ar")
+        def subtract(i):
+            stage, pair, half = UNITS[i]
+            if stage == 0:
+                z = y4[half][pair // 2][:, :, pair % 2 : 4 : 2].rearrange("p n t -> p t n")
+            else:
+                z = y1[half][pair][:]
+            arg = work.tile([P, 2, 2, HALF], F32, name="arg", tag="arg")
             for w in range(2):
-                nc.vector.tensor_tensor(out=ar[:, w], in0=live["ps", i][w][:], in1=y_view(i), op=ALU.subtract)
-            live["ar", i] = ar
+                nc.vector.tensor_tensor(out=arg[:, w], in0=live["products", i][w][:], in1=z, op=ALU.subtract)
+            live["arg", i] = arg
 
-        def exps(i):
-            st, pr, hf = units[i]
+        def column(pair, j):
+            return slice(4 * (pair // 2) + pair % 2 + 2 * j, 4 * (pair // 2) + pair % 2 + 2 * j + 1)
+
+        def exponentials(i):
+            pair = UNITS[i][1]
             ex = work.tile([P, 2, 2, HALF], F32, name="ex", tag="ex")
             for w in range(2):
                 for j in range(2):
-                    slot = 4 * (pr // 2) + pr % 2 + 2 * j
-                    nc.scalar.activation(
-                        ex[:, w, j], live["ar", i][:, w, j], ACT.Exp, bias=vec_f[1 + w][:, slot : slot + 1]
-                    )
+                    nc.scalar.activation(ex[:, w, j], live["arg", i][:, w, j], ACT.Exp, bias=vec_f[1 + w][:, column(pair, j)])
             live["ex", i] = ex
 
-        def difference(i, eng):
-            st, pr, hf = units[i]
+        def first_sum(i, engine):
+            stage, pair, half = UNITS[i]
             ex = live["ex", i]
-            if st == 0:
-                eng.tensor_tensor(out=k1h[hf][pr][:], in0=ex[:, 0], in1=ex[:, 1], op=ALU.subtract)
+            if stage == 0:
+                engine.tensor_tensor(out=k1_half[half][pair][:], in0=ex[:, 0], in1=ex[:, 1], op=ALU.subtract)
             else:
-                tt = work.tile([P, 2, HALF], F32, name="tt", tag="tt")
-                eng.tensor_tensor(out=tt[:], in0=k1h[hf][pr][:], in1=ex[:, 0], op=ALU.add)
-                live["tt", i] = tt
+                part = work.tile([P, 2, HALF], F32, name="part", tag="part")
+                engine.tensor_tensor(out=part[:], in0=k1_half[half][pair][:], in1=ex[:, 0], op=ALU.add)
+                live["part", i] = part
 
-        def finish_v(i):
-            st, pr, hf = units[i]
-            grp = pr // 2
-            if st == 0:
+        def finish(i):
+            stage, pair, half = UNITS[i]
+            grp = pair // 2
+            if stage == 0:
+                bank = live["y_bank", half, grp][:].bitcast(BF16).rearrange("p u (n e) -> p e u n", e=2)
                 nc.vector.scalar_tensor_tensor(
-                    out=y1[hf][pr][:], in0=k1h[hf][pr][:], scalar=0.4, in1=y_psum(i), op0=ALU.mult, op1=ALU.add
+                    out=y1[half][pair][:],
+                    in0=k1_half[half][pair][:],
+                    scalar=0.4,
+                    in1=bank[:, pair % 2],
+                    op0=ALU.mult,
+                    op1=ALU.add,
                 )
                 return
-            if pr % 2 == 0:
-                live["o", hf, grp] = work.tile([P, 2, 4, P], F32, name="o", tag="o")
-            o = live["o", hf, grp]
-            if i != LAST:
-                nc.vector.tensor_tensor(
-                    out=o[:, :, pr % 2 : 4 : 2, :],
-                    in0=live["tt", i][:].rearrange("p j (r n) -> p r j n", r=2),
-                    in1=live["ex", i][:, 1].rearrange("p j (r n) -> p r j n", r=2),
-                    op=ALU.subtract,
-                )
-                return
-            tt = work.tile([P, 2, 2, P], F32, name="tl", tag="tt")
+            if pair % 2 == 0:
+                live["out", half, grp] = work.tile([P, 2, 4, P], F32, name="out_t", tag="out_t")
+            out_t = live["out", half, grp][:, :, pair % 2 : 4 : 2, :]
             ex = live["ex", i][:].rearrange("p w j (r n) -> p w r j n", r=2)
-            kk = k1h[hf][pr][:].rearrange("p j (r n) -> p r j n", r=2)
-            for r in range(2):
-                nc.vector.tensor_tensor(out=tt[:, r], in0=kk[:, r], in1=ex[:, 0, r], op=ALU.add)
-            for r in range(2):
-                nc.vector.tensor_tensor(out=o[:, r, pr % 2 : 4 : 2, :], in0=tt[:, r], in1=ex[:, 1, r], op=ALU.subtract)
-
-        def finish_s(i):
-            st, pr, hf = units[i]
-            grp = pr // 2
-            if st == 0:
-                if pr % 2 == 0:
-                    live["u1s", hf, grp] = work.tile([P, 2, HALF, 2], BF16, name="u1s", tag="u1s", align_bytes=64)
-                for j in range(2):
-                    slot = 4 * grp + pr % 2 + 2 * j
-                    nc.scalar.activation(
-                        live["u1s", hf, grp][:, j, :, pr % 2], y1[hf][pr][:, j, :], ACT.Copy, scale=vec_f[0][:, slot : slot + 1]
-                    )
-            elif pr % 2 == 1:
-                o = live["o", hf, grp]
-                for r in range(2):
-                    bank = psum_t.tile([P, 4, P], F32, name="obank", tag="tr")
-                    for t in range(4):
-                        nc.tensor.transpose(bank[:, t, :], o[:, r, t, :], ident[:])
-                    orow = work.tile([P, P, 4], F32, name="orow", tag="orow", bufs=6)
-                    nc.scalar.copy(out=orow[:], in_=bank[:].rearrange("p t m -> p m t"))
-                    r0 = HALF * hf + P * r
-                    c0 = 512 * grp
-                    (nc.scalar if i == LAST and r == 1 else nc.sync).dma_start(
-                        out=out_0[r0 : r0 + P, c0 : c0 + 512], in_=orow[:].rearrange("p m t -> p (m t)")
-                    )
-
-        def interleave(i, on_scalar):
-            st, pr, hf = units[i]
-            ui = work.tile([P, HALF, 4], BF16, name="ui", tag="u_i", align_bytes=64)
-            copy = nc.scalar.copy if on_scalar else nc.vector.tensor_copy
-            if st == 0:
-                copy(
-                    out=ui[:].rearrange("p n t -> p (n t)").bitcast(F32).rearrange("p (n u) -> p n u", u=2),
-                    in_=live["u1s", hf, pr // 2][:].rearrange("p u n e -> p u (n e)").bitcast(F32).rearrange("p u n -> p n u"),
-                )
-            else:
-                copy(
-                    out=ui[:].rearrange("p (r n) t -> p r n t", r=2),
-                    in_=live["o", hf, pr // 2][:].rearrange("p r t n -> p r n t"),
-                )
-            live["ui", i] = ui
-
-        def quantize_unit(i):
-            st, pr, hf = units[i]
-            t0 = HALF * hf
-            grp = pr // 2
-            ui = live["ui", i][:].rearrange("p n t -> p (n t)")
-            if st == 0:
-                nc.vector.quantize_mx(out=codes[1][hf][:, grp, :].bitcast(FP8X4), scales=scales[1][hf][:, grp, :], in_=ui)
+            if i < LAST:
+                part = live["part", i][:].rearrange("p j (r n) -> p r j n", r=2)
+                nc.vector.tensor_tensor(out=out_t, in0=part, in1=ex[:, 1], op=ALU.subtract)
                 return
-            oc = work.tile([P, HALF], U32, name="oc", tag="oc", align_bytes=64)
-            nc.vector.quantize_mx(out=oc[:].bitcast(FP8X4), scales=out_sc[:, grp, t0 : t0 + HALF], in_=ui)
-            nc.sync.dma_start(out=out_words[grp][:, 4 * t0 : 4 * (t0 + HALF)].bitcast(I32), in_=oc[:].bitcast(I32))
+            part = work.tile([P, 2, 2, P], F32, name="last_part", tag="part")
+            k1_r = k1_half[half][pair][:].rearrange("p j (r n) -> p r j n", r=2)
+            for r in range(2):
+                nc.vector.tensor_tensor(out=part[:, r], in0=k1_r[:, r], in1=ex[:, 0, r], op=ALU.add)
+            for r in range(2):
+                nc.vector.tensor_tensor(out=out_t[:, r], in0=part[:, r], in1=ex[:, 1, r], op=ALU.subtract)
+
+        def scale_by_s(i):
+            _, pair, half = UNITS[i]
+            grp = pair // 2
+            if pair % 2 == 0:
+                live["u1", half, grp] = work.tile([P, 2, HALF, 2], BF16, name="u1", tag="u1", align_bytes=64)
+            for j in range(2):
+                nc.scalar.activation(
+                    live["u1", half, grp][:, j, :, pair % 2],
+                    y1[half][pair][:, j, :],
+                    ACT.Copy,
+                    scale=vec_f[0][:, column(pair, j)],
+                )
+
+        def store_rows(i):
+            _, pair, half = UNITS[i]
+            grp = pair // 2
+            for r in range(2):
+                bank = psum_t.tile([P, 4, P], F32, name="out_bank", tag="tr")
+                for t in range(4):
+                    nc.tensor.transpose(bank[:, t, :], live["out", half, grp][:, r, t, :], ident[:])
+                rows = work.tile([P, P, 4], F32, name="rows", tag="rows", bufs=6)
+                nc.scalar.copy(out=rows[:], in_=bank[:].rearrange("p t m -> p m t"))
+                row0 = HALF * half + P * r
+                (nc.scalar if i == LAST and r == 1 else nc.sync).dma_start(
+                    out=out_0[row0 : row0 + P, GROUP * grp : GROUP * (grp + 1)], in_=rows[:].rearrange("p m t -> p (m t)")
+                )
+
+        def lay_out(i):
+            stage, pair, half = UNITS[i]
+            laid = work.tile([P, HALF, 4], BF16, name="laid", tag="laid", align_bytes=64)
+            copy = nc.scalar.copy if i in LAID_OUT_BY_SCALAR else nc.vector.tensor_copy
+            if stage == 0:
+                u1 = live["u1", half, pair // 2][:].rearrange("p u n e -> p u (n e)").bitcast(F32)
+                copy(out=as_words(laid[:]), in_=u1.rearrange("p u n -> p n u"))
+            else:
+                out_t = live["out", half, pair // 2][:].rearrange("p r t n -> p r n t")
+                copy(out=laid[:].rearrange("p (r n) t -> p r n t", r=2), in_=out_t)
+            live["laid", i] = laid
+
+        def quantize_group(i):
+            stage, pair, half = UNITS[i]
+            grp = pair // 2
+            laid = live["laid", i][:].rearrange("p n t -> p (n t)")
+            if stage == 0:
+                nc.vector.quantize_mx(out=codes[1][half][:, grp, :].bitcast(FP8X4), scales=scales[1][half][:, grp, :], in_=laid)
+                return
+            tokens = slice(HALF * half, HALF * (half + 1))
+            out_codes = work.tile([P, HALF], U32, name="out_codes", tag="out_codes", align_bytes=64)
+            nc.vector.quantize_mx(out=out_codes[:].bitcast(FP8X4), scales=out_scales[:, grp, tokens], in_=laid)
+            nc.sync.dma_start(
+                out=out_words[grp][:, 4 * HALF * half : 4 * HALF * (half + 1)].bitcast(I32), in_=out_codes[:].bitcast(I32)
+            )
             if i == LAST:
                 for q in range(4):
                     nc.sync.dma_start(
                         out=out_2[:, 4 * q : 4 * q + 4, :].rearrange("g r n -> r g n").bitcast(I32),
-                        in_=out_sc[32 * q : 32 * q + 4, :, :].bitcast(I32),
+                        in_=out_scales[32 * q : 32 * q + 4, :, :].bitcast(I32),
                     )
 
-        permute_words(0, 0)
-        permute_words(0, 1)
+        make_identity(nc, ident[:])
+        load_vector(nc.gpsimd, 1)
+        load_vector(nc.gpsimd, 2)
+        for w in range(2):
+            nc.vector.memset(scale_raw[w][:].rearrange("p k n -> p (k n)").bitcast(I32), 0)
+        nc.vector.memset(warm[:], 0.0)
+        nc.scalar.activation(warm[:], warm[:], ACT.Exp)
+        load_words(0, 0)
+        load_vector(nc.sync, 0)
         for grp in range(2):
-            head_t(0, grp)
-        permute_words(1, 0)
-        head_q(0)
-        fin = [i + LAG.get(i, 2) for i in range(n_units)]
-        fin_s = [fin[i] + SX.get(i, 0) for i in range(n_units)]
-        inter = {i: fin[i] + (0 if i in ON_S else 1) + IX.get(i, 0) for i in range(1, n_units, 2)}
-        quant = {i: inter[i] + 1 for i in inter}
-        mul = [i - 2 for i in range(n_units)]
-        for i in range(8, n_units):
-            mul[i] = max(i - 2, max(quant[j] for j in ((1, 3) if i < 12 else (5, 7))))
-        permute_scales(0, 0)
-        if HEAD:
-            permute_words(1, 1)
-        permute_scales(1, 0)
+            load_y(0, grp)
+        load_scales(0)
+        load_words(1, 0)
+        load_scales(1)
+        for grp in range(2):
+            load_y(1, grp)
+        for w in range(2):
+            load_words(w, 1)
+
+        order_words(0, 0)
+        order_words(0, 1)
+        for grp in range(2):
+            transpose_y(0, grp)
+        quantize_u(0)
+        order_scales(0, 0)
+        order_words(1, 0)
+        order_words(1, 1)
+        order_scales(1, 0)
         vectors()
         multiply(0)
-        if not HEAD:
-            permute_words(1, 1)
         multiply(1)
-        for i in range(n_units + 9):
-            if i < n_units:
-                subtract_y(i)
-                exps(i)
-                if i != LAST and i not in ON_V:
-                    difference(i, nc.gpsimd)
-            if i == 0:
+
+        finish_step = [i + FINISH_LAG.get(i, 2) for i in range(len(UNITS))]
+        whole = [i for i, unit in enumerate(UNITS) if unit[1] % 2 == 1]
+        layout_step = {i: finish_step[i] + (0 if i in LAID_OUT_BY_SCALAR else 1) for i in whole}
+        store_step = {i: finish_step[i] + (0 if i == LAST else 1) for i in whole if UNITS[i][0] == 1}
+        for step in range(layout_step[LAST] + 2):
+            if step <= LAST:
+                subtract(step)
+                exponentials(step)
+                if 0 < step < LAST:
+                    first_sum(step, nc.gpsimd)
+            if step == 0:
                 for w in range(2):
-                    permute_scales(w, 1)
-                    permute_words(w, 2)
-            if i == 1:
+                    order_scales(w, 1)
+                    order_words(w, 2)
+            if step == 1:
                 for w in range(2):
-                    permute_words(w, 3)
+                    order_words(w, 3)
                 for grp in range(2):
-                    head_t(1, grp)
-            if i == 2:
-                head_q(1)
-            for j in range(n_units):
-                if fin[j] == i:
-                    if j in ON_V:
-                        difference(j, nc.vector)
-                    finish_v(j)
-                if fin_s[j] == i:
-                    finish_s(j)
-            for j in inter:
-                if quant[j] == i:
-                    quantize_unit(j)
-                if inter[j] == i:
-                    interleave(j, j in ON_S)
-            for j in range(2, n_units):
-                if mul[j] == i:
-                    multiply(j)
+                    transpose_y(1, grp)
+            if step == 2:
+                quantize_u(1)
+            for i in range(len(UNITS)):
+                if finish_step[i] == step:
+                    if i == 0:
+                        first_sum(i, nc.vector)
+                    finish(i)
+                    if UNITS[i][0] == 0:
+                        scale_by_s(i)
+                if store_step.get(i) == step:
+                    store_rows(i)
+            for i in whole:
+                if layout_step[i] + 1 == step:
+                    quantize_group(i)
+                if layout_step[i] == step:
+                    lay_out(i)
+            if step + 2 <= LAST:
+                multiply(step + 2)

import math
from contextlib import ExitStack

import concourse.mybir as mybir
from concourse.masks import make_identity

F32 = mybir.dt.float32
BF16 = mybir.dt.bfloat16
I32 = mybir.dt.int32
U32 = mybir.dt.uint32
U8 = mybir.dt.uint8
FP8X4 = mybir.dt.float8_e4m3fn_x4
FP4X4 = mybir.dt.float4_e2m1fn_x4
ACT = mybir.ActivationFunctionType
ALU = mybir.AluOpType

FLOPS = 4 * 2 * 512 * 1024 * 1024

P = 128
HALF = 256
GROUP = 512

UNITS = [(stage, pair, half) for stage in range(2) for half in range(2) for pair in range(4)]
LAST = len(UNITS) - 1

FINISH_LAG = {0: 1, 9: 1}

LAID_OUT_BY_SCALAR = (3, 7, 11)


def tile_ssystemlogheunslope_x2_kernel(
    tc, y, s, g_words, g_scales, h_words, h_scales, la, lb, out_0, out_1, out_2
):
    nc = tc.nc
    out_words = out_1.rearrange("g p m t -> g p (m t)")

    with ExitStack() as ctx:
        keep = ctx.enter_context(tc.tile_pool(name="keep", bufs=1))
        work = ctx.enter_context(tc.tile_pool(name="work", bufs=3))
        psum = ctx.enter_context(tc.psum_pool(name="psum", bufs=2))
        psum_t = ctx.enter_context(tc.psum_pool(name="psum_t", bufs=4))
        ctx.enter_context(tc.manual_schedule())

        def grid(name, shape, dtype, *dims):
            if not dims:
                return keep.tile(shape, dtype, name=name, align_bytes=64)
            return [grid("%s_%d" % (name, i), shape, dtype, *dims[1:]) for i in range(dims[0])]

        warm = grid("warm", [P, 1], F32)
        ident = grid("ident", [P, P], F32)
        vec = grid("vec", [P, 4, 4], BF16, 3)
        vec_f = grid("vec_f", [P, 8], F32, 3)
        y_tok = grid("y_tok", [P, 2, GROUP], BF16, 2, 2)
        y4 = grid("y4", [P, HALF, 4], BF16, 2, 2)
        word_raw = grid("word_raw", [P, 2, 2 * GROUP], U8, 2, 2)
        words = grid("words", [P, 2, 2, 2 * P], U8, 2, 4)
        scale_raw = grid("scale_raw", [P, 2, 1024], U8, 2)
        scale_w = grid("scale_w", [P, 2, 4, P], U8, 2, 2)
        codes = grid("codes", [P, 2, HALF], U32, 2, 2)
        scales = grid("scales", [P, 2, HALF], U8, 2, 2)
        k1_half = grid("k1_half", [P, 2, HALF], F32, 2, 4)
        y1 = grid("y1", [P, 2, HALF], F32, 2, 4)
        out_scales = grid("out_scales", [P, 2, 512], U8)
        live = {}

        def load_y(half, grp):
            nc.sync.dma_start(
                out=y_tok[half][grp][:],
                in_=y[HALF * half : HALF * (half + 1), GROUP * grp : GROUP * (grp + 1)].rearrange("(r p) k -> p r k", p=P),
            )

        def load_words(w, grp):
            nc.sync.dma_start(
                out=word_raw[w][grp][:].bitcast(I32),
                in_=(g_words, h_words)[w][:, :, 2 * GROUP * grp : 2 * GROUP * (grp + 1)].rearrange("k p b -> p k b").bitcast(I32),
            )

        def load_scales(w):
            for q in range(4):
                nc.sync.dma_start(
                    out=scale_raw[w][32 * q : 32 * q + 4, :, :].bitcast(I32),
                    in_=(g_scales, h_scales)[w][:, 4 * q : 4 * q + 4, :].rearrange("k r n -> r k n").bitcast(I32),
                )

        def load_vector(queue, a):
            queue.dma_start(out=vec[a][:, 0:2], in_=(s, la, lb)[a].rearrange("(g p t) -> p g t", p=P, t=4))

        def vectors():
            for a in (1, 2):
                nc.vector.tensor_scalar_add(vec_f[a][:], vec[a][:, 0:2].rearrange("p g t -> p (g t)"), math.log(0.5))
            nc.vector.tensor_copy(out=vec_f[0][:], in_=vec[0][:, 0:2].rearrange("p g t -> p (g t)"))

        def as_words(tile):
            return tile.rearrange("p n t -> p (n t)").bitcast(F32).rearrange("p (n u) -> p n u", u=2)

        def transpose_y(half, grp):
            bank = psum_t.tile([P, 2, HALF], F32, name="y_bank", tag="tr")
            for r in range(2):
                rows = y_tok[half][grp][:, r, :].bitcast(F32)
                for u in range(2):
                    nc.tensor.transpose(bank[:, u, P * r : P * (r + 1)], rows[:, u : GROUP // 2 : 2], ident[:])
            live["y_bank", half, grp] = bank
            if grp == 0:
                live["u", half] = work.tile([P, 2, HALF, 4], BF16, name="u", tag="u", align_bytes=64)
            nc.vector.tensor_tensor(
                out=live["u", half][:, grp].rearrange("p n (u e) -> p n u e", e=2),
                in0=bank[:].bitcast(BF16).rearrange("p u (n e) -> p n u e", e=2),
                in1=vec[0][:, grp, :].rearrange("p (u e) -> p u e", e=2).unsqueeze(1).to_broadcast([P, HALF, 2, 2]),
                op=ALU.mult,
            )
            nc.scalar.copy(out=as_words(y4[half][grp][:]), in_=bank[:].rearrange("p u n -> p n u"))

        def quantize_u(half):
            nc.vector.quantize_mx(
                out=codes[0][half][:].rearrange("p g n -> p (g n)").bitcast(FP8X4),
                scales=scales[0][half][:].rearrange("p g n -> p (g n)"),
                in_=live["u", half][:].rearrange("p g n t -> p (g n t)"),
            )

        def order_words(w, pair):
            src = word_raw[w][pair // 2][:].rearrange("p k (m t b) -> p k t m b", t=4, b=2)
            nc.vector.tensor_copy(
                out=words[w][pair][:].rearrange("p k t (m b) -> p k t m b", b=2), in_=src[:, :, pair % 2 : 4 : 2]
            )

        def order_scales(w, grp):
            src = scale_raw[w][:].rearrange("p k (g m t) -> p k g t m", g=2, t=4)
            nc.vector.tensor_copy(out=scale_w[w][grp][:], in_=src[:, :, grp])

        def multiply(i):
            stage, pair, half = UNITS[i]
            banks = []
            for w in range(2):
                bank = psum.tile([P, 2, HALF], F32, name="product%d" % w, tag="product%d" % w)
                for j in range(2):
                    for r in range(2):
                        cols = slice(P * r, P * (r + 1))
                        for k in range(2):
                            nc.tensor.matmul_mx(
                                out=bank[:, j, cols],
                                lhsT=words[w][pair][:, k, j, :].bitcast(FP4X4),
                                lhsT_scale=scale_w[w][pair // 2][:, k, pair % 2 + 2 * j, :],
                                rhs=codes[stage][half][:, k, cols].bitcast(FP8X4),
                                rhs_scale=scales[stage][half][:, k, cols],
                                start=(k == 0),
                                stop=(k == 1),
                            )
                banks.append(bank)
            live["products", i] = banks

        def subtract(i):
            stage, pair, half = UNITS[i]
            if stage == 0:
                z = y4[half][pair // 2][:, :, pair % 2 : 4 : 2].rearrange("p n t -> p t n")
            else:
                z = y1[half][pair][:]
            arg = work.tile([P, 2, 2, HALF], F32, name="arg", tag="arg")
            for w in range(2):
                nc.vector.tensor_tensor(out=arg[:, w], in0=live["products", i][w][:], in1=z, op=ALU.subtract)
            live["arg", i] = arg

        def column(pair, j):
            return slice(4 * (pair // 2) + pair % 2 + 2 * j, 4 * (pair // 2) + pair % 2 + 2 * j + 1)

        def exponentials(i):
            pair = UNITS[i][1]
            ex = work.tile([P, 2, 2, HALF], F32, name="ex", tag="ex")
            for w in range(2):
                for j in range(2):
                    nc.scalar.activation(ex[:, w, j], live["arg", i][:, w, j], ACT.Exp, bias=vec_f[1 + w][:, column(pair, j)])
            live["ex", i] = ex

        def first_sum(i, engine):
            stage, pair, half = UNITS[i]
            ex = live["ex", i]
            if stage == 0:
                engine.tensor_tensor(out=k1_half[half][pair][:], in0=ex[:, 0], in1=ex[:, 1], op=ALU.subtract)
            else:
                part = work.tile([P, 2, HALF], F32, name="part", tag="part")
                engine.tensor_tensor(out=part[:], in0=k1_half[half][pair][:], in1=ex[:, 0], op=ALU.add)
                live["part", i] = part

        def finish(i):
            stage, pair, half = UNITS[i]
            grp = pair // 2
            if stage == 0:
                bank = live["y_bank", half, grp][:].bitcast(BF16).rearrange("p u (n e) -> p e u n", e=2)
                nc.vector.scalar_tensor_tensor(
                    out=y1[half][pair][:],
                    in0=k1_half[half][pair][:],
                    scalar=0.4,
                    in1=bank[:, pair % 2],
                    op0=ALU.mult,
                    op1=ALU.add,
                )
                return
            if pair % 2 == 0:
                live["out", half, grp] = work.tile([P, 2, 4, P], F32, name="out_t", tag="out_t")
            out_t = live["out", half, grp][:, :, pair % 2 : 4 : 2, :]
            ex = live["ex", i][:].rearrange("p w j (r n) -> p w r j n", r=2)
            if i < LAST:
                part = live["part", i][:].rearrange("p j (r n) -> p r j n", r=2)
                nc.vector.tensor_tensor(out=out_t, in0=part, in1=ex[:, 1], op=ALU.subtract)
                return
            part = work.tile([P, 2, 2, P], F32, name="last_part", tag="part")
            k1_r = k1_half[half][pair][:].rearrange("p j (r n) -> p r j n", r=2)
            for r in range(2):
                nc.vector.tensor_tensor(out=part[:, r], in0=k1_r[:, r], in1=ex[:, 0, r], op=ALU.add)
            for r in range(2):
                nc.vector.tensor_tensor(out=out_t[:, r], in0=part[:, r], in1=ex[:, 1, r], op=ALU.subtract)

        def scale_by_s(i):
            _, pair, half = UNITS[i]
            grp = pair // 2
            if pair % 2 == 0:
                live["u1", half, grp] = work.tile([P, 2, HALF, 2], BF16, name="u1", tag="u1", align_bytes=64)
            for j in range(2):
                nc.scalar.activation(
                    live["u1", half, grp][:, j, :, pair % 2],
                    y1[half][pair][:, j, :],
                    ACT.Copy,
                    scale=vec_f[0][:, column(pair, j)],
                )

        def store_rows(i):
            _, pair, half = UNITS[i]
            grp = pair // 2
            for r in range(2):
                bank = psum_t.tile([P, 4, P], F32, name="out_bank", tag="tr")
                for t in range(4):
                    nc.tensor.transpose(bank[:, t, :], live["out", half, grp][:, r, t, :], ident[:])
                rows = work.tile([P, P, 4], F32, name="rows", tag="rows", bufs=6)
                nc.scalar.copy(out=rows[:], in_=bank[:].rearrange("p t m -> p m t"))
                row0 = HALF * half + P * r
                (nc.scalar if i == LAST and r == 1 else nc.sync).dma_start(
                    out=out_0[row0 : row0 + P, GROUP * grp : GROUP * (grp + 1)], in_=rows[:].rearrange("p m t -> p (m t)")
                )

        def lay_out(i):
            stage, pair, half = UNITS[i]
            laid = work.tile([P, HALF, 4], BF16, name="laid", tag="laid", align_bytes=64)
            copy = nc.scalar.copy if i in LAID_OUT_BY_SCALAR else nc.vector.tensor_copy
            if stage == 0:
                u1 = live["u1", half, pair // 2][:].rearrange("p u n e -> p u (n e)").bitcast(F32)
                copy(out=as_words(laid[:]), in_=u1.rearrange("p u n -> p n u"))
            else:
                out_t = live["out", half, pair // 2][:].rearrange("p r t n -> p r n t")
                copy(out=laid[:].rearrange("p (r n) t -> p r n t", r=2), in_=out_t)
            live["laid", i] = laid

        def quantize_group(i):
            stage, pair, half = UNITS[i]
            grp = pair // 2
            laid = live["laid", i][:].rearrange("p n t -> p (n t)")
            if stage == 0:
                nc.vector.quantize_mx(out=codes[1][half][:, grp, :].bitcast(FP8X4), scales=scales[1][half][:, grp, :], in_=laid)
                return
            tokens = slice(HALF * half, HALF * (half + 1))
            out_codes = work.tile([P, HALF], U32, name="out_codes", tag="out_codes", align_bytes=64)
            nc.vector.quantize_mx(out=out_codes[:].bitcast(FP8X4), scales=out_scales[:, grp, tokens], in_=laid)
            nc.sync.dma_start(
                out=out_words[grp][:, 4 * HALF * half : 4 * HALF * (half + 1)].bitcast(I32), in_=out_codes[:].bitcast(I32)
            )
            if i == LAST:
                for q in range(4):
                    nc.sync.dma_start(
                        out=out_2[:, 4 * q : 4 * q + 4, :].rearrange("g r n -> r g n").bitcast(I32),
                        in_=out_scales[32 * q : 32 * q + 4, :, :].bitcast(I32),
                    )

        make_identity(nc, ident[:])
        load_vector(nc.gpsimd, 1)
        load_vector(nc.gpsimd, 2)
        for w in range(2):
            nc.vector.memset(scale_raw[w][:].rearrange("p k n -> p (k n)").bitcast(I32), 0)
        nc.vector.memset(warm[:], 0.0)
        nc.scalar.activation(warm[:], warm[:], ACT.Exp)
        load_words(0, 0)
        load_vector(nc.sync, 0)
        for grp in range(2):
            load_y(0, grp)
        load_scales(0)
        load_words(1, 0)
        load_scales(1)
        for grp in range(2):
            load_y(1, grp)
        for w in range(2):
            load_words(w, 1)

        order_words(0, 0)
        order_words(0, 1)
        for grp in range(2):
            transpose_y(0, grp)
        quantize_u(0)
        order_scales(0, 0)
        order_words(1, 0)
        order_words(1, 1)
        order_scales(1, 0)
        vectors()
        multiply(0)
        multiply(1)

        finish_step = [i + FINISH_LAG.get(i, 2) for i in range(len(UNITS))]
        whole = [i for i, unit in enumerate(UNITS) if unit[1] % 2 == 1]
        layout_step = {i: finish_step[i] + (0 if i in LAID_OUT_BY_SCALAR else 1) for i in whole}
        store_step = {i: finish_step[i] + (0 if i == LAST else 1) for i in whole if UNITS[i][0] == 1}
        for step in range(layout_step[LAST] + 2):
            if step <= LAST:
                subtract(step)
                exponentials(step)
                if 0 < step < LAST:
                    first_sum(step, nc.gpsimd)
            if step == 0:
                for w in range(2):
                    order_scales(w, 1)
                    order_words(w, 2)
            if step == 1:
                for w in range(2):
                    order_words(w, 3)
                for grp in range(2):
                    transpose_y(1, grp)
            if step == 2:
                quantize_u(1)
            for i in range(len(UNITS)):
                if finish_step[i] == step:
                    if i == 0:
                        first_sum(i, nc.vector)
                    finish(i)
                    if UNITS[i][0] == 0:
                        scale_by_s(i)
                if store_step.get(i) == step:
                    store_rows(i)
            for i in whole:
                if layout_step[i] + 1 == step:
                    quantize_group(i)
                if layout_step[i] == step:
                    lay_out(i)
            if step + 2 <= LAST:
                multiply(step + 2)
